import numpy as np, ml_dtypes
CORES = [10,34,74,98]
N = 4
BF = ml_dtypes.bfloat16
def gentries(a):
    return np.ascontiguousarray(a.reshape(8, 16, -1).transpose(0, 2, 1)).reshape(8, -1)
def gtable(e):
    e = np.asarray(e); return np.ascontiguousarray(e.reshape(8, -1, 16).transpose(0, 2, 1)).reshape(128, -1).astype(np.int32)
V, S0, C, T = 4096, 256, 64, 4
A, B = (12, 13, 12, 14), (10, 11, 9, 11)
S = S0 + C * T
K = 64
def first(m):
    return np.take_along_axis(m, np.argmax(m < V, axis=-1)[..., None], -1)[..., 0]
def parts(rng):
    n, h = V // K, S0 // K
    vp = np.argsort(rng.random((8, V)), axis=1); w = np.full((N, 8, K, 16 * h), V); w[..., :n] = vp.reshape(8, K, n)
    m = np.take_along_axis(w, np.argsort(rng.random(w.shape), axis=-1), -1).reshape(N, 8, S0, 16)
    s = np.arange(S0)[:, None]; pos = s // h * n
    up = s + ((S0 - s) * rng.random(m.shape)).astype(np.int64); j = pos + ((V - pos) * rng.random(m.shape)).astype(np.int64)
    e1 = np.take_along_axis(first(m), up.reshape(N, 8, -1), 2).reshape(m.shape)
    e2 = np.take_along_axis(np.broadcast_to(vp, (N, 8, V)), j.reshape(N, 8, -1), 2).reshape(m.shape)
    z = rng.random(m.shape)
    return vp, m, np.where(z < 0.45, e1, np.where(z < 0.75, e2, np.where(z < 0.95, rng.integers(0, V, m.shape), V)))
def steps(rng, vp, dev, down):
    u = np.arange(K) + rng.integers(0, 24, (N, 8, 16, K)); cl = np.argsort(vp, axis=1) // (V // K)
    ix = np.take_along_axis(u, cl[None, :, None, :], 3) + 4
    i = np.arange(16)[:, None]; off = (i * (2 * rng.integers(0, 8, dev.shape) + 1) + rng.integers(0, 16, dev.shape)) % 16 < dev
    d = -1 if down else rng.integers(1, 4, ix.shape) * (2 * rng.integers(0, 2, ix.shape) - 1)
    return ix + np.where(off, d, 0)
def pack(rng, tab, ix, m, e):
    o = np.argsort(rng.random((N, 8, S0)), axis=2)[..., None]; e = np.where(np.any(m < V, axis=3, keepdims=True), e, V)
    m = np.take_along_axis(m, o, 2); e = np.take_along_axis(e, o, 2)
    return {"xs": np.take_along_axis(tab, ix, 3).astype(np.float32).reshape(N, 128, V).astype(BF),
            "mem0": np.stack([gtable(a.reshape(8, -1)) for a in m]), "inv0": np.stack([gtable(a.reshape(8, -1)) for a in e])}
def plain(rng):
    return np.sort(rng.standard_normal((N, 8, 16, 128)), axis=3) * np.exp2(rng.integers(-2, 3, (N, 8, 16, 1)))
def even(rng):
    return (np.arange(128) - 50) * np.exp2(rng.integers(-2, 3, (N, 8, 16, 1)))
def some(rng, share):
    return np.where(rng.random((N, 8, 1, V)) < share, rng.integers(1, 17, (N, 8, 1, V)), 0)
def chain(rng, vp, m, e, dev):
    n, h = V // K, S0 // K
    a = np.full((K, h, 16), V); a[:, :n // 16] = vp[7].reshape(K, n // 16, 16); a = a.reshape(S0, 16)
    s, row = np.argwhere(a == 0)[0]; a[s, row] = a[s, 1]; a[s, 1] = 0
    full = np.flatnonzero(a[:, 0] < V); sp = np.append(rng.permutation(full[full != s])[:C // 8 - 1], s)
    c = np.stack([np.append([0, 15], rng.permutation(np.arange(1, 15))) for b in sp]) ^ int(rng.integers(0, 16))
    m[:, 7] = a; dev[:, 7] = 0
    for q in range(N): dev[q, 7, 0, a[sp]] = 16 * ((c >> (q % 4)) & 1)
    z = rng.random((N, S0, 16))
    e[:, 7] = np.where(z < 0.5, a[:, :1], np.where(z < 0.75, rng.choice(a[sp, 0], z.shape), e[:, 7])); e[:, 7, :, 2] = a[:, 0]
def setup_inputs(rng):
    vp, m, e = parts(rng); share = rng.choice(np.array([0.004, 0.01, 0.02, 0.05]), (N, 8, 1, 1))
    return pack(rng, plain(rng), steps(rng, vp, some(rng, share), False), m, e)
def setup_inputs_room(rng):
    vp, m, e = parts(rng); dev = np.zeros((N, 8, 1, V), np.int64)
    for q in range(1, N, 2):
        for g in range(8):
            a = m[q - 1, g]; can = np.flatnonzero(np.sum(a < V, axis=1) > 1); row = np.argmax((a < V) * (rng.random(a.shape) + 0.5), axis=1)
            n = (C, C + 1, C - 1, S0, 1, 0, C, 2)[g] if q == 1 else int(rng.choice(np.array([0, 1, 2, C - 1, C, C + 1, S0])))
            s = rng.permutation(can)[:n]; dev[q, g, 0, a[s, row[s]]] = 16
    return pack(rng, even(rng), steps(rng, vp, dev, False), m, e)
def setup_inputs_ties(rng):
    vp, m, e = parts(rng); n, h = V // K, S0 // K
    j = np.arange(S0)[:, None] // h * n + rng.integers(0, n, m.shape)
    own = np.take_along_axis(np.broadcast_to(vp, (N, 8, V)), j.reshape(N, 8, -1), 2).reshape(m.shape)
    e = np.where(rng.random(m.shape) < 0.8, own, e); z = rng.random((N, 8, 1, V)); t = rng.integers(0, T, z.shape); one = rng.integers(0, 2, z.shape)
    dev = np.where(z < 0.02, 16 - np.array(B)[t] + one, np.where(z < 0.3, 16 - np.array(A)[t] + one, 0))
    chain(rng, vp, m, e, dev)
    return pack(rng, even(rng), steps(rng, vp, dev, True), m, e)
def setup_inputs_alike(rng):
    vp, m, e = parts(rng)
    m = np.where(rng.random(m.shape) < rng.random((N, 8, S0, 1)) * 1.2, m, V); m[:, :, 3::7, :15] = V; m[:, :, 5::11] = V
    lead = first(m); e[:, ::2] = rng.choice(np.array([0, V - 1, V // 2, V]), (N, 4, S0, 16))
    e[:, 1] = lead[:, 1, :, None]; e[:, 3] = lead[:, 3, S0 // 2, None, None]; e[:, 5] = V
    return pack(rng, plain(rng), steps(rng, vp, some(rng, 0.1), False), m, e)
def setup_inputs_crowd(rng):
    vp, m, e = parts(rng); share = rng.choice(np.array([0.1, 0.3, 0.8]), (N, 8, 1, 1)); share[rng.integers(0, N)] = 0.0; share[:, rng.integers(0, 8)] = 0.0
    return pack(rng, plain(rng), steps(rng, vp, some(rng, share), False), m, e)
def setup_inputs_spread(rng):
    vp, m, e = parts(rng); share = rng.choice(np.array([0.004, 0.01, 0.02, 0.05]), (N, 8, 1, 1)); w = (N, 8, 16, 128)
    z = rng.standard_normal(w); z = z * (np.abs(z) > 2.0 ** -8)
    size = np.exp2(rng.choice(np.array([-65, -62, -40, -20, -2, 0, 2, 20, 40, 80]), (N, 8, 16, 1)))
    tab = np.sort(z * np.exp2(rng.integers(-6, 7, w)) * (rng.random(w) > 0.0625), axis=3) * size
    return pack(rng, tab, steps(rng, vp, some(rng, share), False), m, e)
def check_inputs(d):
    bad = []
    x = np.abs(d["xs"].astype(np.float32))
    if not np.all((x == 0) | ((x >= 2.0 ** -100) & (x <= 2.0 ** 100))): bad.append("sizes of the numbers in xs")
    for k in ("mem0", "inv0"):
        if np.min(d[k]) < 0 or np.max(d[k]) > V: bad.append("range of " + k)
    z = np.sort(np.stack([gentries(a) for a in d["mem0"]]), axis=2)
    if np.any((z[..., 1:] == z[..., :-1]) & (z[..., 1:] < V)): bad.append("no variable twice in a group of mem0")
    a, b = d["mem0"].reshape(-1, 8, 16, S0), d["inv0"].reshape(-1, 8, 16, S0)
    if np.any(np.any(b < V, axis=2) & ~np.any(a < V, axis=2)): bad.append("no bounds in slots without members")
    return bad
def reference(xs, mem0, inv0):
    x = np.concatenate([xs.astype(np.float32).reshape(N, 8, 16, V), np.zeros((N, 8, 16, 1), np.float32)], axis=3)
    M = np.full((N, 8, S, 16), V, np.int64); I = np.full((N, 8, S, 16), V, np.int64)
    for r in range(N):
        M[r, :, :S0] = gentries(mem0[r]).reshape(8, S0, 16); I[r, :, :S0] = gentries(inv0[r]).reshape(8, S0, 16)
    for t in range(T):
        n = S0 + C * t
        for r in range(N):
            w = x[(r + t) % N]; m = M[r, :, :n].copy(); e = I[r, :, :n].copy(); lead = first(m)
            xl = np.take_along_axis(w, lead[:, None, :], 2)[..., None]
            xm = np.take_along_axis(w, m.reshape(8, 1, -1), 2).reshape(8, 16, n, 16); xe = np.take_along_axis(w, e.reshape(8, 1, -1), 2).reshape(8, 16, n, 16)
            e = np.where(np.sum(xl <= xe, axis=1) < A[t], V, e)
            leave = (m < V) & (np.sum(xm == xl, axis=1) < B[t])
            has = np.any(leave, axis=2).astype(np.int64); before = np.add.accumulate(has, axis=1) - has
            split = (has == 1) & (before < C); leave = leave & split[..., None]
            stay = np.where(leave, V, m); go = np.where(leave, m, V)
            M[r, :, :n] = stay; I[r, :, :n] = e
            for g in range(8):
                ids = np.flatnonzero(split[g]); k = len(ids)
                f = np.arange(V + 1); f[lead[g, ids]] = first(go[g, ids])
                M[r, g, n:n + k] = go[g, ids]; I[r, g, n:n + k] = np.where(e[g, ids] < V, f[e[g, ids]], stay[g, ids])
    return {"ym": np.stack([gtable(a.reshape(8, -1)) for a in M]).astype(np.float32), "yi": np.stack([gtable(a.reshape(8, -1)) for a in I]).astype(np.float32)}

@@ -1,0 +1,574 @@
+from concourse.mybir import AluOpType as A, AxisListType, ActivationFunctionType as F
+
+V, S0, C, NT = 4096, 256, 64, 4
+TA, TB = (12, 13, 12, 14), (10, 11, 9, 11)
+ROWS = {(0, None): 12, (1, None): 12, (1, 0): 12, (2, None): 12, (2, 0): 8, (2, 1): 12,
+        (3, None): 12, (3, 0): 12, (3, 1): 8, (3, 2): 12}
+IDS_S = [4, 4, 4, 4]
+ON_S = {"gw": 0, "nz": 0, "hv": 1, "dead": 1, "inv": 0}
+FG_V = [24, 0, 0, 32]
+XW = 4176
+BIG = 8192.0
+EPS = 2.0 ** -115
+
+TSW, NW = 528, 208
+U_TS = [TSW * t for t in range(4)]
+U_NEW = {}
+_c = 4 * TSW
+for _t in range(1, 4):
+    for _j in range(_t):
+        U_NEW[(_t, _j)] = _c
+        _c += NW
+U_M = [_c + 512 * t for t in range(5)]
+_c += 512 * 5
+U_E = [_c + 512 * t for t in range(5)]
+_c += 512 * 5
+UW = _c
+O_NEW = [NW * t for t in range(4)]
+O_M = [4 * NW + 512 * t for t in range(4)]
+O_E = [4 * NW + 2048 + 512 * t for t in range(4)]
+OW = 4 * NW + 4096
+CW = 31 * 448
+
+SCRATCH = {
+    "xw": ("sbuf", [128, XW], "bfloat16"), "ft": ("sbuf", [128, XW], "bfloat16"),
+    "mi": ("sbuf", [128, 256], "int32"), "ei": ("sbuf", [128, 256], "int32"),
+    "uin": ("sbuf", [128, UW], "uint16"), "uout": ("sbuf", [128, OW], "uint16"),
+    "ts0": ("sbuf", [128, TSW], "uint16"),
+    "cmp": ("sbuf", [128, 2 * CW], "bfloat16"), "xe": ("sbuf", [128, 2 * 16 * 448], "bfloat16"),
+    "xl": ("sbuf", [128, 4 * 1280], "bfloat16"),
+    "mw": ("sbuf", [128, 2048], "float32"), "ein": ("sbuf", [128, 2048], "float32"), "ew": ("sbuf", [128, 2048], "float32"),
+    "ww": ("sbuf", [128, 2048], "bfloat16"), "hb": ("sbuf", [128, 2048], "bfloat16"), "cum": ("sbuf", [128, 512], "bfloat16"),
+    "inv": ("sbuf", [128, 1024], "bfloat16"), "junk": ("sbuf", [128, 2048], "bfloat16"),
+    "acc": ("sbuf", [128, 8], "float32"), "ids": ("sbuf", [128, 32], "uint16"), "lt": ("sbuf", [128, 64], "uint16"),
+    "g1": ("sbuf", [128, 2, 64], "float32"), "g2": ("sbuf", [128, 64], "float32"),
+    "gs": ("sbuf", [128, 10 * 64], "float32"),
+    "tp": ("sbuf", [128, 768], "float32"), "nz": ("sbuf", [128, 256], "float32"), "sc": ("sbuf", [128, 256], "float32"),
+    "xx": ("sbuf", [128, 128], "float32"), "hv": ("sbuf", [128, 320], "bfloat16"),
+    "fo": ("sbuf", [128, 64], "uint16"), "fg": ("sbuf", [128, 1024], "bfloat16"),
+    "mf": ("sbuf", [128, 512], "float32"), "ef": ("sbuf", [128, 448], "float32"),
+    "lasti": ("sbuf", [128, 64], "float32"), "lasto": ("sbuf", [128, 64], "float32"),
+    "pi": ("sbuf", [128, 1], "int32"), "ci": ("sbuf", [128, 8], "int32"), "cf": ("sbuf", [128, 32], "float32"),
+    "jf": ("sbuf", [128, 160], "float32"), "jg": ("sbuf", [128, 128], "float32"), "jc": ("sbuf", [128, 64], "float32"),
+    "jx": ("sbuf", [128, 8], "float32"),
+    "b1": ("sbuf", [128, 144], "bfloat16"), "b8": ("sbuf", [128, 144], "bfloat16"), "b4": ("sbuf", [128, 144], "bfloat16"),
+    "bf": ("sbuf", [128, 144], "float32"), "ea": ("sbuf", [128, 128], "float32"),
+    "idb": ("sbuf", [128, 128], "bfloat16"), "idn": ("sbuf", [128, 128], "bfloat16"), "idf": ("sbuf", [128, 128], "float32"),
+    "bo": ("sbuf", [128, 128], "bfloat16"), "rr": ("sbuf", [128, 288], "float32"),
+    "dg": ("sbuf", [128, 512], "bfloat16"), "dr": ("sbuf", [128, 512], "bfloat16"),
+    "ones": ("sbuf", [128, 448], "bfloat16"), "zero": ("sbuf", [128, 128], "bfloat16"),
+    "fake": ("sbuf", [128, 64], "float32"), "pm": ("sbuf", [128, 128], "float32"), "ol": ("sbuf", [128, 32], "uint16"),
+}
+PS = ["pm0", "pm1", "pe0", "pe1", "pd0", "pd1", "pd2", "pd3"]
+for _n in PS:
+    SCRATCH[_n] = ("psum", [128, 16, 32], "float32")
+
+MSG = ["ts1", "ts2", "ts3"] + ["%s%d" % (k, t) for t in range(3) for k in "abcd"] + ["f02", "f03", "f13", "b3", "c3", "d3"]
+SEMAPHORES = ["qv", "qs", "qp", "qg", "sent"] + ["r_" + m for m in MSG] + ["l%d" % k for k in range(7)]
+QSEM = {"V": "qv", "S": "qs", "P": "qp", "G": "qg"}
+
+CY, PCY, GA, SCA = 0.00104, 0.00055, 1.56, 3.5
+T_SEM, T_HOP, T_RISS, T_DMA = 0.08, 5.0, 0.5, 2.0
+DBW = 300.0
+LOOK = 0.1
+SEED, JIT, PASSES = 2791, 0.0, 4
+
+
+def build(T, topo, core, rank):
+    ops = []
+
+    def sb(name, a=0, b=None, step=None):
+        w = T[name].shape[1]
+        b = w if b is None else b
+        return (T[name][:, a:b] if step is None else T[name][:, a:b:step], (name, a, b), len(range(a, b, step or 1)))
+
+    def v3(name, a, b, h=None):
+        t = T[name][:, a // 32:b // 32, :] if h is None else T[name][:, a // 32:b // 32, 16 * h:16 * h + 16]
+        return (t, (name, a, b), (b - a) // (1 if h is None else 2))
+
+    def ind(win, off):
+        return (win[0].indirect(off[0]), [win[1], off[1]], 16 * off[2], "ind")
+
+    def regs(xs):
+        out = []
+        for x in xs:
+            if isinstance(x, tuple):
+                out += x[1] if isinstance(x[1], list) else [x[1]]
+        return out
+
+    def val(x):
+        return x[0] if isinstance(x, tuple) else x
+
+    def two(*xs):
+        return all(SCRATCH[r[0]][2] in ("bfloat16", "uint16") for r in regs(xs))
+
+    def add(q, fn, outs, ins, cost, **kw):
+        rd, wr = regs(ins), regs(outs)
+        for o in outs:
+            if len(o) == 4:
+                wr.remove(o[1][1]); rd.append(o[1][1])
+        d = dict(q=q, fn=fn, rd=rd, wr=wr, cost=cost, lat=0.0, id=len(ops), deps={}, grp=None, acc=False, tok=None)
+        d.update(kw)
+        ops.append(d)
+        return d
+
+    def vcost(out, first, k):
+        if len(out) == 4: return 0.05 + out[2] * SCA * CY
+        if len(first) == 4: return 0.05 + first[2] * GA * CY
+        return 0.05 + max(64, first[2] * k) * CY
+
+    def cp(out, a):
+        return add("V", lambda g: g.vector.tensor_copy(out[0], a[0]), [out], [a], vcost(out, a, 0.5 if two(out, a) else 1))
+
+    def ts(out, a, s1, o1, s2=None, o2=None):
+        if o2 is None: fn = lambda g: g.vector.tensor_scalar(out[0], a[0], val(s1), None, o1)
+        else: fn = lambda g: g.vector.tensor_scalar(out[0], a[0], val(s1), val(s2), o1, o2)
+        return add("V", fn, [out], [a, s1, s2], vcost(out, a, 0.5 if two(out, a) else 1))
+
+    def tt(out, a, b, o):
+        k = 1 if any(r[0] in PS for r in regs([a, b])) else 2
+        return add("V", lambda g: g.vector.tensor_tensor(out[0], a[0], b[0], o), [out], [a, b], vcost(out, a, k))
+
+    def scan(out, a, b, o0, o1):
+        return add("V", lambda g: g.vector.tensor_tensor_scan(out[0], a[0], b[0], 0.0, o0, o1), [out], [a, b],
+                   vcost(out, a, 0.5 if two(out, a, b) else 1))
+
+    def red(out, a):
+        return add("V", lambda g: g.vector.tensor_reduce(out[0], a[0], AxisListType.X, A.add), [out], [a], vcost(out, a, 1))
+
+    def tr(out, a):
+        return add("V", lambda g: g.vector.transpose(out[0], a[0]), [out], [a], vcost(out, a, 1))
+
+    def act(out, a, f, bias=0.0, scale=1.0, acc=None):
+        if acc is None: fn = lambda g: g.scalar.activation(out[0], a[0], f, bias=val(bias), scale=val(scale))
+        else: fn = lambda g: g.scalar.activation(out[0], a[0], f, bias=val(bias), scale=val(scale), accum_out=acc[0])
+        cost = 0.065 + (a[2] * GA if len(a) == 4 else max(64, a[2])) * CY
+        return add("S", fn, [out] + ([acc] if acc else []), [a, bias, scale], cost)
+
+    def mm(out, l, r, grp, first=False):
+        k = 4 if SCRATCH[l[1][0]][2] == "float32" else 1
+        d = add("P", None, [out], [l, r], 0.02 + max(64, r[2]) * k * PCY, grp=grp, acc=not first)
+        d["mm"] = (out[0], l[0], r[0], first)
+        return d
+
+    def iota(out, pat, base, cm):
+        if SCRATCH[out[1][0]][2] == "int32": fn = lambda g: g.iota(out[0], pat, base, cm)
+        else: fn = lambda g: g.iota(out[0], pat, base, cm, allow_small_or_imprecise_dtypes=True)
+        return add("G", fn, [out], [], 0.13 + 2 * out[2] * CY)
+
+    nl = [0]
+
+    def dma(q, out, a, kb):
+        s = "l%d" % nl[0]; nl[0] += 1
+        if q == "Y": fn = lambda g: g.sync.dma_start(val(out), val(a)).then_inc(T.sem[s], 16)
+        else: fn = lambda g: g.scalar.dma_start(val(out), val(a)).then_inc(T.sem[s], 16)
+        outs = [out] if isinstance(out, tuple) else []
+        return add(q, fn, outs, [a], 0.06, lat=T_DMA + kb / DBW, tok=(s, 16))
+
+    def send(src, dests, kb):
+        for k, land, m in dests:
+            c = T.cores[(rank + k) % len(T.cores)]
+            back = T.cores[(rank - k) % len(T.cores)]
+            rid, pid, _ = topo.addr(c)
+            fn = (lambda land, m, rid, pid, mk: lambda g: g.remote_dma(land[0], src[0], T.sem["r_" + m], T.sem.sent, pid, rid, mk))(
+                land, m, rid, pid, topo.mask(core, c))
+            s = add("G", fn, [], [src], T_RISS, tok="none", sent=len(topo.engines(core, c)))
+            r = add("R", None, [land], [], 0.0, lat=T_HOP + kb / 80.0, tok=("r_" + m, len(topo.engines(back, core))))
+            r["after"] = s["id"]
+
+    col = lambda k: sb("cf", k, k + 1)
+    E = lambda name, i: sb(name, 15 - i, 143 - i)
+
+    dma("Y", sb("mi"), T.mem0[:], 128)
+    dma("S", sb("ei"), T.inv0[:], 128)
+    dma("Y", sb("xw", 0, 2048), T.xs[:, 0:2048], 700)
+    dma("S", sb("xw", 2048, 4096), T.xs[:, 2048:4096], 1000)
+    iota(sb("pi"), [[0, 1]], 0, 1)
+    iota(sb("jf"), [[1, 160]], 0, 0)
+    for k, m in enumerate((15, 112, 96, 16, 1, 12, 2, 7)):
+        ts(sb("ci", k, k + 1), sb("pi"), m, A.bitwise_and)
+    cp(sb("cf", 0, 6), sb("ci", 0, 6))
+    cp(sb("cf", 28, 30), sb("ci", 6, 8))
+    ts(col(6), col(2), col(0), A.subtract, 31.0, A.add)
+    ts(col(7), col(3), 0.0, A.is_equal)
+    ts(col(8), col(3), 0.0, A.is_gt)
+    for e in range(2):
+        ts(sb("rr", 144 * e, 144 * e + 144), sb("jf", 0, 144), col(6), A.is_equal, col(7 + e), A.mult)
+    ts(col(30), col(0), 2.0, A.mult, 15.0, A.add)
+    ts(col(9), col(29), 30.0, A.mult, col(30), A.add)
+    ts(sb("ol", 0, 16), sb("jf", 0, 16), -1.0, A.mult, col(9), A.add)
+    ts(col(31), col(28), 8.0, A.mult, 15.0, A.add)
+    ts(col(10), col(4), 32.0, A.mult, col(31), A.add)
+    ts(col(11), col(5), -0.25, A.mult, col(10), A.add)
+    ts(sb("ol", 16, 20), sb("jf", 0, 4), -4.0, A.mult, col(11), A.add)
+    cp(sb("ol", 20, 21), col(10))
+    iota(sb("jx"), [[64, 2], [16, 2], [32, 2]], 15, 0)
+    cp(sb("ol", 24, 32), sb("jx"))
+    ts(sb("b1"), sb("jf", 0, 144), col(1), A.subtract, 15.0, A.is_equal)
+    act(sb("b8"), sb("b1"), F.Copy, scale=BIG)
+    act(sb("b4"), sb("b1"), F.Copy, scale=BIG / 2)
+    act(sb("bf"), sb("b1"), F.Copy)
+    tt(sb("ea"), E("bf", 0), E("bf", 1), A.subtract)
+    cp(col(12), sb("pi"))
+    ts(sb("idb"), sb("jf", 0, 128), col(12), A.is_equal)
+    act(sb("idn"), sb("idb"), F.Copy, scale=-1.0)
+    act(sb("idf"), sb("idb"), F.Copy)
+    iota(sb("xw", 4096, XW), [[0, XW - 4096]], 0, 0)
+    iota(sb("zero"), [[0, 128]], 0, 0)
+    iota(sb("ones"), [[0, 448]], 1, 0)
+    iota(sb("jg"), [[16, 8], [0, 16]], 0, 0)
+    iota(sb("jc"), [[0, 4], [1, 16]], 0, 0)
+    ts(sb("bo"), sb("jg"), col(1), A.is_equal)
+    ts(sb("cf", 16, 20), sb("jf", 0, 64, 16), col(0), A.add, 0.5, A.add)
+    dr = {}
+    for k, r in enumerate(sorted(set(ROWS.values()) - {0})):
+        dr[r] = sb("dr", 128 * k, 128 * k + 128)
+        ts(col(24 + k), col(0), float(r), A.is_lt, 8 * BIG, A.mult)
+        act(dr[r], sb("idb"), F.Copy, scale=col(24 + k))
+    ts(col(14), col(0), 15.0, A.is_equal)
+    ts(sb("fake"), sb("jf", 0, 64), V + 1.0, A.add, col(14), A.mult)
+    ts(sb("pm", 0, 64), sb("jc"), col(0), A.is_equal)
+    act(sb("pm", 64, 128), sb("pm", 0, 64), F.Copy, scale=-1.0)
+    wb, db = {}, {}
+    for t in range(NT):
+        if TB[t] not in wb:
+            wb[TB[t]] = col(20 + t)
+            ts(col(20 + t), col(0), 0.0, A.is_gt, BIG * TB[t], A.mult)
+        if TA[t] not in db:
+            db[TA[t]] = sb("dg", 128 * t, 128 * t + 128)
+            act(db[TA[t]], sb("idb"), F.Copy, scale=BIG * (1 - TA[t]))
+        n = S0 + C * t
+        for nm, c in (("mw", 0), ("ew", 0), ("ww", 0), ("hb", 1)):
+            iota(sb(nm, 512 * t + n, 512 * t + n + 64), [[0, 64]], c, 0)
+    for k in range(8):
+        iota(sb("ft", k * (XW // 8), (k + 1) * (XW // 8)), [[0, XW // 8]], 0, 0)
+
+    def arrange(ps, w, half, grp):
+        for e in range(2):
+            for h in range(2):
+                mm(v3(ps, 0, w, e), sb("rr", 144 * e + 16 - 16 * h, 144 * e + 144 - 16 * h), half(h), grp + (e,), h == 0)
+
+    ts(sb("mw", 0, 256), sb("mi"), -1.0, A.mult, float(V), A.add)
+    arrange("pd2", 256, lambda h: sb("mw", 128 * h, 128 * h + 128), ("sm",))
+    tr(sb("tp", 0, 256), v3("pd2", 0, 256))
+    act(sb("nz"), sb("tp", 0, 256), F.Relu, bias=1.0, scale=-1.0)
+    scan(sb("sc"), sb("nz"), sb("tp", 0, 256), A.mult, A.add)
+    ts(sb("ts0", 512, 528), ind(sb("sc"), sb("ol", 0, 1)), -1.0, A.mult, float(V), A.add)
+    ts(sb("ts0", 0, 256), ind(sb("tp", 0, 256), sb("ol", 0, 16)), -1.0, A.mult, float(V), A.add)
+    ts(sb("ein", 0, 256), sb("ei"), -1.0, A.mult, float(V), A.add)
+    arrange("pd3", 256, lambda h: sb("ein", 128 * h, 128 * h + 128), ("se",))
+    tr(sb("tp", 256, 512), v3("pd3", 0, 256))
+    ts(sb("ts0", 256, 512), ind(sb("tp", 256, 512), sb("ol", 0, 16)), -1.0, A.mult, float(V), A.add)
+    send(sb("ts0", 16, TSW), [(k, sb("uin", U_TS[k] + 16, U_TS[k] + TSW), "ts%d" % k) for k in (1, 2, 3)], 128)
+
+    xwin = sb("xw", 0, XW)
+    bank = [0, 0]
+
+    def compare(t, j, part):
+        par = t % 2
+        if j is None:
+            nm, u, w, c0, x0, rep = ("ts0", 0, 256, 0, 0, 2) if t == 0 else ("uin", U_TS[t], 256, 0, 0, 2)
+            um, ue, ul, lw = u, u + 256, u + 512, 16
+        else:
+            nm, u, w, c0, x0, rep = "uin", U_NEW[(t, j)], 64, S0 + C * j, 512 + 256 * j, 4
+            um, ue, ul, lw = u, u + 80, u + 64, 16
+        k = w // 16
+        x0 += 1280 * t
+        cb = CW * par + 31 * c0
+        if part == "m":
+            act(sb("xl", x0, x0 + 256), ind(xwin, sb(nm, ul, ul + lw)), F.Copy)
+            if j is None: act(sb("xl", x0 + 256, x0 + 512), sb("xl", x0, x0 + 256), F.Copy)
+            i = 1
+            while i < 16:
+                i2 = min(16, (i // rep + 1) * rep)
+                o = cb + (i - 1) * w
+                tt(sb("cmp", o, o + (i2 - i) * w), ind(xwin, sb(nm, um + k * i, um + k * i2)), sb("xl", x0, x0 + (i2 - i) * w), A.is_equal)
+                for r in range(i, i2):
+                    mm(v3("pm%d" % par, c0, c0 + w), E("b1", r), sb("cmp", cb + (r - 1) * w, cb + r * w), ("m", t))
+                i = i2
+            return
+        cb += 15 * w
+        i = 0
+        newest = j is not None and j == t - 1
+        R0 = ROWS[(t, j)]
+        if R0: mm(v3("pe%d" % par, c0, c0 + w), dr[R0], sb("ones", 0, w), ("e", t))
+        while i < R0:
+            i2 = min(R0, i + 512 // w)
+            ln = (i2 - i) * w
+            xo = 16 * 448 * par + 16 * c0 + i * w
+            act(sb("xe", xo, xo + ln), ind(xwin, sb(nm, ue + k * i, ue + k * i2)), F.Copy)
+            b = 1 if newest else 0
+            pd = "pd%d" % (2 * b + bank[b] % 2); bank[b] += 1
+            grp = ("d", t, j, i)
+            mm(v3(pd, 0, ln), sb("idb"), sb("xe", xo, xo + ln), grp, True)
+            for o in range(0, ln, rep * w):
+                o2 = min(ln, o + rep * w)
+                mm(v3(pd, o, o2), sb("idn"), sb("xl", x0, x0 + o2 - o), grp)
+            act(sb("cmp", cb + i * w, cb + i2 * w), v3(pd, 0, ln), F.Sign, bias=EPS)
+            for r in range(i, i2):
+                mm(v3("pe%d" % par, c0, c0 + w), E("b4", r), sb("cmp", cb + r * w, cb + (r + 1) * w), ("e", t))
+            i = i2
+        while i < 16:
+            i2 = min(16, i + rep)
+            tt(sb("cmp", cb + i * w, cb + i2 * w), ind(xwin, sb(nm, ue + k * i, ue + k * i2)), sb("xl", x0, x0 + (i2 - i) * w), A.is_ge)
+            for r in range(i, i2):
+                mm(v3("pe%d" % par, c0, c0 + w), E("b8", r), sb("cmp", cb + r * w, cb + (r + 1) * w), ("e", t))
+            i = i2
+
+    def early(t):
+        n, par = S0 + C * t, t % 2
+        mm(v3("pm%d" % par, 0, n), sb("zero"), sb("ones", 0, n), ("m", t), True)
+        mm(v3("pe%d" % par, 0, n), db[TA[t]], sb("ones", 0, n), ("e", t), True)
+        for j in [None] + list(range(t - 1)):
+            compare(t, j, "m")
+            compare(t, j, "e")
+
+    def decide(t):
+        n, par, b = S0 + C * t, t % 2, 512 * t
+        N = n + 64
+        pm, pe = "pm%d" % par, "pe%d" % par
+        gs = lambda k: sb("gs", 64 * k, 64 * k + 64) if k != 2 else sb("gs", 64 * (2, 7, 8, 9)[t], 64 * (2, 7, 8, 9)[t] + 64)
+        ns, i0, lt, hv = IDS_S[t], 8 * t, sb("lt", 16 * t, 16 * t + 4), sb("hv", 64 + 64 * t, 128 + 64 * t)
+        iv = sb("inv", 512 * par, 512 * par + n)
+        if t == 0:
+            act(iv, sb("mw", 0, 256), F.Relu, bias=16.0, scale=-16.0)
+        else:
+            cp(sb("mw", b, b + n), sb("uin", U_M[t], U_M[t] + n))
+            if ON_S["inv"]: act(iv, sb("mw", b, b + n), F.Relu, bias=16.0, scale=-16.0)
+            else: ts(iv, sb("uin", U_M[t], U_M[t] + n), 0.0, A.is_equal, 16.0, A.mult)
+            compare(t, t - 1, "m")
+            cp(sb("ein", b, b + n - 64), sb("uin", U_E[t], U_E[t] + n - 64))
+            u = U_NEW[(t, t - 1)]
+            cp(sb("ein", b + n - 64, b + n), sb("uin", u + 144, u + 208))
+            compare(t, t - 1, "e")
+        mm(v3(pm, 0, n), sb("idb"), iv, ("m", t))
+        act(sb("ww", b, b + n), v3(pm, 0, n), F.Relu, bias=wb[TB[t]], scale=-BIG)
+        mm(v3(pm, 0, n), sb("bo"), sb("ww", b, b + n), ("h", t), True)
+        act(sb("hb", b, b + n), v3(pm, 0, n), F.Sign)
+        scan(sb("cum", 0, N), sb("hb", b, b + N), sb("hb", b, b + N), A.add, A.max)
+        for d in range(4):
+            jk = sb("junk", 512 * d, 512 * d + N)
+            if d < ns:
+                act(jk, sb("cum", 0, N), F.Sign, bias=col(16 + d), scale=-1.0, acc=sb("acc", d, d + 1))
+            else:
+                ts(jk, sb("cum", 0, N), col(16 + d), A.is_le)
+                red(sb("acc", d, d + 1), jk)
+        if ns < 4: cp(sb("ids", i0 + ns, i0 + 4), sb("acc", ns, 4))
+        if ns > 0: ts(sb("ids", i0, i0 + ns), sb("acc", 0, ns), float(N), A.add, 0.5, A.mult)
+        ids = sb("ids", i0, i0 + 4)
+        mwin, ewin, wwin = sb("mw", b, b + N), sb("ew", b, b + N), sb("ww", b, b + N)
+        go, mfk = (T.g1[:, 0], ("g1", 0, 64), 64), (T.g1[:, 1], ("g1", 64, 128), 64)
+        if ON_S["gw"]: act(gs(0), ind(wwin, ids), F.Copy)
+        else: cp(gs(0), ind(wwin, ids))
+        tt(go, ind(mwin, ids), gs(0), A.min)
+        tt(mfk, ind(mwin, ids), sb("fake"), A.max)
+        act(gs(1), ind(mwin, ids), F.Copy)
+        arrange(pm, 128, lambda h: (T.g1[:, :, 32 * h:32 * h + 32], ("g1", 0, 128), 64), ("a1", t))
+        tr(sb("tp", 512, 640), v3(pm, 0, 128))
+        if ON_S["nz"]: act(sb("nz", 0, 128), sb("tp", 512, 640), F.Relu, bias=1.0, scale=-1.0)
+        else: ts(sb("nz", 0, 128), sb("tp", 512, 640), 0.0, A.is_equal)
+        scan(sb("sc", 0, 128), sb("nz", 0, 128), sb("tp", 512, 640), A.mult, A.add)
+        o = O_NEW[t]
+        if t < 3:
+            ts(sb("uout", o, o + 64), ind(sb("tp", 512, 576), sb("ol", 16, 20)), -1.0, A.mult, float(V), A.add)
+            ts(sb("uout", o + 64, o + 80), ind(sb("sc", 0, 64), sb("ol", 20, 21)), -1.0, A.mult, float(V), A.add)
+            u = U_NEW[(t + 1, t)]
+            send(sb("uout", o + 4, o + 80), [(1, sb("uin", u + 4, u + 80), "a%d" % t)], 19)
+        tt(gs(2), gs(1), go, A.subtract)
+        cp(ind(mwin, ids), gs(2))
+        cp(sb("uout", O_M[t], O_M[t] + n), sb("mw", b, b + n))
+        cp(sb("uout", O_M[t] + n, O_M[t] + N), go)
+        send(sb("uout", O_M[t], O_M[t] + N), [(1, sb("uin", U_M[t + 1], U_M[t + 1] + N), "b%d" % t)], N / 4)
+        tt(sb("xx"), ind(sb("sc", 0, 128), sb("ol", 24, 32)), sb("pm"), A.mult)
+        cp(sb("lt", 16 * t, 16 * t + 16), ind(sb("sc", 64, 128), sb("ol", 20, 21)))
+        mm(v3(pm, 128, 192), sb("ea"), sb("xx", 0, 64), ("ta", t), True)
+        mm(v3(pm, 128, 192), sb("ea"), sb("xx", 64, 128), ("ta", t))
+        mm(v3(pm, 192, 256), E("bf", 1), sb("xx", 0, 64), ("tb", t), True)
+        mm(v3(pm, 192, 256), E("bf", 1), sb("xx", 64, 128), ("tb", t))
+        if ON_S["hv"]: act(sb("hv", 0, 64), v3(pm, 128, 192), F.Copy)
+        else: cp(sb("hv", 0, 64), v3(pm, 128, 192))
+        tt(hv, sb("hv", 0, 64), v3(pm, 192, 256), A.add)
+        cp(ind(sb("ft"), lt), hv)
+        tt(sb("ew", b, b + n), sb("ein", b, b + n), v3(pe, 0, n), A.min)
+        cp(sb("uout", O_E[t], O_E[t] + n), sb("ew", b, b + n))
+        send(sb("uout", O_E[t], O_E[t] + n), [(1, sb("uin", U_E[t + 1], U_E[t + 1] + n), "c%d" % t)], n / 4)
+        act(gs(3), ind(ewin, ids), F.Relu)
+        if ON_S["dead"]: act(gs(4), ind(ewin, ids), F.Relu, bias=BIG, scale=-BIG)
+        else: ts(gs(4), ind(ewin, ids), 0.0, A.is_le, BIG, A.mult)
+        tt(gs(5), gs(4), gs(2), A.min)
+        if t < 3:
+            tt(sb("g2"), gs(3), gs(5), A.subtract)
+            arrange("pd2", 64, lambda h: sb("g2", 32 * h, 32 * h + 32), ("a2", t))
+            tr(sb("tp", 640, 704), v3("pd2", 0, 64))
+            cp(sb("fo"), ind(sb("tp", 640, 704), sb("ol", 16, 20)))
+            act(gs(6), ind(sb("tp", 640, 704), sb("ol", 16, 20)), F.Abs)
+        else:
+            cp(sb("fo"), ind(ewin, ids))
+        fv = FG_V[t]
+        if fv: cp(sb("fg", 0, 16 * fv), ind(sb("ft"), sb("fo", 0, fv)))
+        if fv < 64: act(sb("fg", 16 * fv, 1024), ind(sb("ft"), sb("fo", fv, 64)), F.Copy)
+        if t < 3:
+            mm(v3("pd3", 0, 64), sb("idf"), gs(6), ("nt", t), True)
+            for c in range(16):
+                mm(v3("pd3", 0, 64), E("b1", c), sb("fg", c, 1024, 16), ("nt", t))
+            ts(sb("uout", o + 80, o + 144), v3("pd3", 0, 64), -1.0, A.mult, float(V), A.add)
+        pn = "pd2"
+        mm(v3(pn, 256, 320), sb("idf"), gs(3), ("nn", t), True)
+        mm(v3(pn, 256, 320), sb("idf"), gs(5), ("nn", t))
+        for i in range(16):
+            mm(v3(pn, 256, 320), E("b1", i), sb("fg", 64 * i, 64 * i + 64) if t < 3 else sb("fg", i, 1024, 16), ("nn", t))
+        if t < 3:
+            cp(sb("uout", o + 144, o + 208), v3(pn, 256, 320))
+            u = U_NEW[(t + 1, t)]
+            send(sb("uout", o + 80, o + 208), [(1, sb("uin", u + 80, u + 208), "d%d" % t)], 32)
+            far = [(k - t, sb("uin", U_NEW[(k, t)] + 4, U_NEW[(k, t)] + 144), "f%d%d" % (t, k)) for k in range(t + 2, 4)]
+            send(sb("uout", o + 4, o + 144), far, 35)
+            cp(ind(sb("ft"), lt), sb("zero", 0, 64))
+        else:
+            ts(sb("lasto"), v3(pn, 256, 320), -1.0, A.mult, float(V), A.add)
+            send(sb("lasto"), [(1, sb("lasti"), "d3")], 32)
+
+    early(0)
+    for t in range(NT):
+        if t + 1 < NT: early(t + 1)
+        decide(t)
+    ts(sb("mf"), sb("uin", U_M[4], U_M[4] + 512), -1.0, A.mult, float(V), A.add)
+    dma("Y", T.ym[:], sb("mf"), 256)
+    ts(sb("ef"), sb("uin", U_E[4], U_E[4] + 448), -1.0, A.mult, float(V), A.add)
+    dma("Y", T.yi[:, 0:448], sb("ef"), 224)
+    dma("Y", T.yi[:, 448:512], sb("lasti"), 32)
+    return ops
+
+
+def link(ops):
+    seen = {}
+    for o in ops:
+        acc = [(r, False) for r in o["rd"]] + [(r, True) for r in o["wr"]]
+        for r, w in acc:
+            ps = r[0] in PS
+            a, b = (0, 1) if ps else r[1:]
+            for (p, pa, pb, pw) in seen.get(r[0], []):
+                if p is o or pb <= a or b <= pa or not (w or pw or ps): continue
+                if p["q"] == "P" and o["q"] == "P":
+                    if p["grp"] != o["grp"] or not p["acc"]: o["deps"][p["id"]] = "order"
+                elif ps and p["q"] == o["q"] and not (w or pw): continue
+                else: o["deps"][p["id"]] = "wait"
+        for r, w in acc:
+            a, b = (0, 1) if r[0] in PS else r[1:]
+            lst = seen.setdefault(r[0], [])
+            if w and not (o["q"] == "P" and o["acc"]):
+                lst[:] = [x for x in lst if not (a <= x[1] and x[2] <= b)]
+            lst.append((o, a, b, w))
+        if "after" in o: o["deps"][o["after"]] = "hop"
+
+
+def one_pass(ops, pred, succ, prio, back):
+    n = len(ops)
+    left = [len(p) for p in pred]
+    ready, free = {}, {}
+    rt, st, fin = [0.0] * n, [0.0] * n, [0.0] * n
+    for i in range(n):
+        if not left[i]:
+            ready.setdefault(ops[i]["q"], []).append(i)
+            if back: rt[i] = ops[i]["lat"]
+    for _ in range(n):
+        best = None
+        for q, lst in ready.items():
+            if not lst: continue
+            t0 = max(free.get(q, 0.0), min(rt[i] for i in lst))
+            i = max((k for k in lst if rt[k] <= t0), key=lambda k: prio[k])
+            for k in lst:
+                if rt[k] > t0 and prio[k] > prio[i] and rt[k] - t0 < LOOK * ops[i]["cost"]: i = k
+            if best is None or t0 < best[0]: best = (t0, max(t0, rt[i]), q, i)
+        _, s, q, i = best
+        ready[q].remove(i)
+        o = ops[i]
+        if q != "R": free[q] = s + o["cost"]
+        st[i], fin[i] = s, s + o["cost"] + (0.0 if back else o["lat"])
+        for k, gap in succ[i]:
+            rt[k] = max(rt[k], fin[i] + gap + (ops[k]["lat"] if back else 0.0))
+            left[k] -= 1
+            if not left[k]: ready.setdefault(ops[k]["q"], []).append(k)
+    return st, fin
+
+
+def schedule(ops):
+    n = len(ops)
+    pred = [[(d, T_SEM if k == "wait" else 0.0) for d, k in o["deps"].items()] for o in ops]
+    succ = [[] for _ in ops]
+    for i in range(n):
+        for d, gap in pred[i]: succ[d].append((i, gap))
+    prio = [0.0] * n
+    for i in reversed(range(n)):
+        prio[i] = ops[i]["cost"] + ops[i]["lat"] + max([prio[s] + gap for s, gap in succ[i]] + [0.0])
+    z, best = SEED, None
+    for _ in range(PASSES):
+        for i in range(n):
+            z = (z * 1103515245 + 12345) % 2147483648
+            prio[i] += JIT * z / 2147483648.0
+        st, fin = one_pass(ops, pred, succ, prio, False)
+        if best is None or max(fin) < best[0]: best = (max(fin), st)
+        prio = one_pass(ops, succ, pred, fin, True)[1]
+    for i in range(n): ops[i]["st"] = best[1][i]
+    return sorted(ops, key=lambda o: (o["st"], o["id"]))
+
+
+def emit(g, T, ops, order):
+    qs = {"V": g.vector, "S": g.scalar, "P": g.tensor, "G": g, "Y": g.sync}
+    pos = {}
+    for k, o in enumerate(order): pos[o["id"]] = k
+    need, lastg = set(), {}
+    for o in order:
+        top = {}
+        for d, kind in o["deps"].items():
+            p = ops[d]
+            if kind == "wait" and p["tok"] is None and (p["q"] not in top or pos[d] > pos[top[p["q"]]]): top[p["q"]] = d
+        need.update(top.values())
+        o["top"] = list(top.values())
+        if o["grp"] is not None: lastg[o["grp"]] = o["id"]
+    cnt = {}
+    for o in order:
+        if o["id"] in need:
+            cnt[o["q"]] = cnt.get(o["q"], 0) + 1
+            o["tok"] = (QSEM[o["q"]], cnt[o["q"]])
+            o["inc"] = True
+    known = {q: {} for q in qs}
+    clock, sent, total = {}, 0, {}
+    for o in order:
+        q = o["q"]
+        if q == "R":
+            clock[o["id"]] = {o["tok"][0]: o["tok"][1]}
+            total[o["tok"][0]] = o["tok"][1]
+            continue
+        kn = known[q]
+        ds = o["top"] + [d for d, kind in o["deps"].items() if kind == "wait" and ops[d]["lat"] > 0]
+        for d in sorted(ds, key=lambda d: -pos[d]):
+            s, v = ops[d]["tok"]
+            if kn.get(s, 0) < v:
+                qs[q].wait_ge(T.sem[s], v)
+                for s2, v2 in clock[d].items(): kn[s2] = max(kn.get(s2, 0), v2)
+        if q == "P":
+            out, l, r, first = o["mm"]
+            ins = g.tensor.matmul(out, l, r, first, lastg[o["grp"]] == o["id"])
+        else:
+            ins = o["fn"](g)
+        ck = dict(kn)
+        if o.get("inc"):
+            ins.then_inc(T.sem[o["tok"][0]], 1)
+        if isinstance(o["tok"], tuple):
+            ck[o["tok"][0]] = o["tok"][1]
+            total[o["tok"][0]] = o["tok"][1]
+        clock[o["id"]] = ck
+        sent += o.get("sent", 0)
+    total["sent"] = sent
+    for s, v in total.items():
+        g.wait_ge(T.sem[s], v)
+
+
+def rank_program(g, core, T, topo):
+    rank = T.rank_of(core)
+    if rank is None:
+        return
+    ops = build(T, topo, core, rank)
+    link(ops)
+    emit(g, T, ops, schedule(ops))

@@ -1,80 +1,94 @@
-from concourse.mybir import AluOpType as A, AxisListType, ActivationFunctionType as F
+import math
+
+from concourse.bass import DstId, RemoteDMATransfer
+from concourse.mybir import AluOpType as A, ActivationFunctionType as F
 
 V, S0, C, NT = 4096, 256, 64, 4
 TA, TB = (12, 13, 12, 14), (10, 11, 9, 11)
-ROWS = {(0, None): 12, (1, None): 12, (1, 0): 12, (2, None): 12, (2, 0): 8, (2, 1): 12,
-        (3, None): 12, (3, 0): 12, (3, 1): 8, (3, 2): 12}
-IDS_S = [4, 4, 4, 4]
-ON_S = {"gw": 0, "nz": 0, "hv": 1, "dead": 1, "inv": 0}
-FG_V = [24, 0, 0, 32]
+VS = 96
+SS = S0 - VS
+ON_V = [True, True, True, True]
+S_PARTS = [(160, 40, (3, 3, 3, 3, 2, 2))]
+V_PART = (VS, VS // 2, (5, 5, 3, 3))
+OLD_GATHER = 32
+V_GATHERS = []
+V_SIGNS = []
+M_RUNS = [(1,) * 5 + (2,) * 5, (1,) + (2,) * 7, (1,) + (2,) * 7, (1,) + (2,) * 7]
+OLD_RUNS = (8, 6)
+FG_V = [0, 0, 0, 32]
 XW = 4176
-BIG = 8192.0
-EPS = 2.0 ** -115
+OFF = 65535.0
+KS = 64.0
 
-TSW, NW = 528, 208
-U_TS = [TSW * t for t in range(4)]
-U_NEW = {}
-_c = 4 * TSW
+TSW = 256 + VS + 256
+U_TS, U_A, _c = {}, {}, 0
+for _t in range(4):
+    U_TS[_t] = _c
+    _c += TSW + C * _t
 for _t in range(1, 4):
     for _j in range(_t):
-        U_NEW[(_t, _j)] = _c
-        _c += NW
+        U_A[(_t, _j)] = _c
+        _c += 64
 U_M = [_c + 512 * t for t in range(5)]
 _c += 512 * 5
-U_E = [_c + 512 * t for t in range(5)]
-_c += 512 * 5
-UW = _c
-O_NEW = [NW * t for t in range(4)]
-O_M = [4 * NW + 512 * t for t in range(4)]
-O_E = [4 * NW + 2048 + 512 * t for t in range(4)]
-OW = 4 * NW + 4096
-CW = 31 * 448
+U_H = _c
+UW = _c + 256
+O_A = [80 * t for t in range(4)]
+O_D = [320 + 64 * t for t in range(4)]
+O_M = [576 + 512 * t for t in range(4)]
+OW = 576 + 2048
+CW = 15 * 256 + 14 * 192 + 16 * 448
+XE = 16 * 448
+XL = 768 + 3 * VS + 3 * 512
+OL_NEW, OL_VS, OL_X = 18, 24, 24 + VS // 16 + VS // 16 % 2
+OLW = OL_X + 4
 
 SCRATCH = {
     "xw": ("sbuf", [128, XW], "bfloat16"), "ft": ("sbuf", [128, XW], "bfloat16"),
     "mi": ("sbuf", [128, 256], "int32"), "ei": ("sbuf", [128, 256], "int32"),
     "uin": ("sbuf", [128, UW], "uint16"), "uout": ("sbuf", [128, OW], "uint16"),
-    "ts0": ("sbuf", [128, TSW], "uint16"),
-    "cmp": ("sbuf", [128, 2 * CW], "bfloat16"), "xe": ("sbuf", [128, 2 * 16 * 448], "bfloat16"),
-    "xl": ("sbuf", [128, 4 * 1280], "bfloat16"),
-    "mw": ("sbuf", [128, 2048], "float32"), "ein": ("sbuf", [128, 2048], "float32"), "ew": ("sbuf", [128, 2048], "float32"),
-    "ww": ("sbuf", [128, 2048], "bfloat16"), "hb": ("sbuf", [128, 2048], "bfloat16"), "cum": ("sbuf", [128, 512], "bfloat16"),
-    "inv": ("sbuf", [128, 1024], "bfloat16"), "junk": ("sbuf", [128, 2048], "bfloat16"),
-    "acc": ("sbuf", [128, 8], "float32"), "ids": ("sbuf", [128, 32], "uint16"), "lt": ("sbuf", [128, 64], "uint16"),
-    "g1": ("sbuf", [128, 2, 64], "float32"), "g2": ("sbuf", [128, 64], "float32"),
-    "gs": ("sbuf", [128, 10 * 64], "float32"),
-    "tp": ("sbuf", [128, 768], "float32"), "nz": ("sbuf", [128, 256], "float32"), "sc": ("sbuf", [128, 256], "float32"),
-    "xx": ("sbuf", [128, 128], "float32"), "hv": ("sbuf", [128, 320], "bfloat16"),
+    "cmp": ("sbuf", [128, 2 * CW], "bfloat16"), "xe": ("sbuf", [128, 2 * XE], "bfloat16"),
+    "xl": ("sbuf", [128, 4 * XL], "bfloat16"),
+    "mw": ("sbuf", [128, 2048], "float32"), "ew": ("sbuf", [128, 2048], "float32"),
+    "ww": ("sbuf", [128, 2048], "bfloat16"), "sg": ("sbuf", [128, 2048], "bfloat16"), "sp": ("sbuf", [128, 2560], "bfloat16"),
+    "hw": ("sbuf", [128, 40], "bfloat16"), "cs": ("sbuf", [128, 160], "bfloat16"), "c2": ("sbuf", [128, 128], "bfloat16"),
+    "fi": ("sbuf", [128, 64], "bfloat16"), "ids": ("sbuf", [128, 64], "uint16"),
+    "g1": ("sbuf", [128, 2, 64], "float32"), "gs": ("sbuf", [128, 192], "float32"),
+    "tp": ("sbuf", [128, 256], "float32"), "t0": ("sbuf", [128, 1024], "float32"),
+    "xx": ("sbuf", [128, 128], "float32"), "hv": ("sbuf", [128, 192], "bfloat16"),
     "fo": ("sbuf", [128, 64], "uint16"), "fg": ("sbuf", [128, 1024], "bfloat16"),
-    "mf": ("sbuf", [128, 512], "float32"), "ef": ("sbuf", [128, 448], "float32"),
-    "lasti": ("sbuf", [128, 64], "float32"), "lasto": ("sbuf", [128, 64], "float32"),
-    "pi": ("sbuf", [128, 1], "int32"), "ci": ("sbuf", [128, 8], "int32"), "cf": ("sbuf", [128, 32], "float32"),
-    "jf": ("sbuf", [128, 160], "float32"), "jg": ("sbuf", [128, 128], "float32"), "jc": ("sbuf", [128, 64], "float32"),
-    "jx": ("sbuf", [128, 8], "float32"),
-    "b1": ("sbuf", [128, 144], "bfloat16"), "b8": ("sbuf", [128, 144], "bfloat16"), "b4": ("sbuf", [128, 144], "bfloat16"),
+    "mf": ("sbuf", [128, 512], "float32"), "ef": ("sbuf", [128, 512], "float32"), "eh": ("sbuf", [128, 448], "float32"),
+    "pi": ("sbuf", [128, 1], "int32"), "ci": ("sbuf", [128, 8], "int32"), "cf": ("sbuf", [128, 16], "float32"),
+    "jf": ("sbuf", [128, 160], "float32"), "jc": ("sbuf", [128, 64], "float32"),
+    "row": ("sbuf", [128, 16 * (OLW + 2)], "bfloat16"), "ol": ("sbuf", [128, OLW + 2], "uint16"),
+    "b1": ("sbuf", [128, 144], "bfloat16"), "b2": ("sbuf", [128, 144], "bfloat16"),
     "bf": ("sbuf", [128, 144], "float32"), "ea": ("sbuf", [128, 128], "float32"),
-    "idb": ("sbuf", [128, 128], "bfloat16"), "idn": ("sbuf", [128, 128], "bfloat16"), "idf": ("sbuf", [128, 128], "float32"),
-    "bo": ("sbuf", [128, 128], "bfloat16"), "rr": ("sbuf", [128, 288], "float32"),
-    "dg": ("sbuf", [128, 512], "bfloat16"), "dr": ("sbuf", [128, 512], "bfloat16"),
-    "ones": ("sbuf", [128, 448], "bfloat16"), "zero": ("sbuf", [128, 128], "bfloat16"),
-    "fake": ("sbuf", [128, 64], "float32"), "pm": ("sbuf", [128, 128], "float32"), "ol": ("sbuf", [128, 32], "uint16"),
+    "idb": ("sbuf", [128, 128], "bfloat16"), "dg": ("sbuf", [128, 9 * 128], "bfloat16"), "df": ("sbuf", [128, 3 * 128], "float32"),
+    "bo": ("sbuf", [128, 4 * 128], "bfloat16"), "rr": ("sbuf", [128, 288], "float32"), "rb": ("sbuf", [128, 288], "bfloat16"),
+    "ones": ("sbuf", [128, 448], "bfloat16"), "neg": ("sbuf", [128, 448], "bfloat16"), "fl": ("sbuf", [128, 256 + 3 * 136], "bfloat16"),
+    "cst": ("sbuf", [128, 448], "bfloat16"), "thr": ("sbuf", [128, 128], "bfloat16"), "seg": ("sbuf", [128, 128], "bfloat16"),
+    "rst": ("sbuf", [128, 160], "bfloat16"), "pm": ("sbuf", [128, 64], "float32"),
 }
-PS = ["pm0", "pm1", "pe0", "pe1", "pd0", "pd1", "pd2", "pd3"]
+PS = ["pm0", "pm1", "pe0", "pe1", "pd0", "pd1", "pd2", "px"]
 for _n in PS:
-    SCRATCH[_n] = ("psum", [128, 16, 32], "float32")
+    SCRATCH[_n] = ("psum", [128, 16, 32] if _n[:2] == "pm" else [128, 512], "float32")
+EPS = 2.0 ** -115
 
-MSG = ["ts1", "ts2", "ts3"] + ["%s%d" % (k, t) for t in range(3) for k in "abcd"] + ["f02", "f03", "f13", "b3", "c3", "d3"]
-SEMAPHORES = ["qv", "qs", "qp", "qg", "sent"] + ["r_" + m for m in MSG] + ["l%d" % k for k in range(7)]
+MSG = ["ts1", "ts2", "ts3"] + ["%s%d" % (k, t) for t in range(3) for k in "abcd"] + ["b3", "c3", "d3"]
+MSG += ["a02", "a03", "d02", "d03", "a13", "d13", "h1", "h2"]
+SEMAPHORES = ["qv", "qs", "qp", "qg", "sent"] + ["r_" + m for m in MSG] + ["l%d" % k for k in range(48)]
 QSEM = {"V": "qv", "S": "qs", "P": "qp", "G": "qg"}
 
-CY, PCY, GA, SCA = 0.00104, 0.00055, 1.56, 3.5
-T_SEM, T_HOP, T_RISS, T_DMA = 0.08, 5.0, 0.5, 2.0
-DBW = 300.0
-LOOK = 0.1
-SEED, JIT, PASSES = 2791, 0.0, 4
+COSTS = [(0.00083, 0.00042, 0.003, 1.56, 3.5, 3.0, 0.5, 0.05, 0.1), (0.001, 0.00053, 0.0, 1.1, 2.5, 2.0, 0.4, 0.03, 0.05),
+         (0.00083, 0.00057, 0.0, 1.5, 3.5, 2.5, 0.6, 0.02, 0.08), (0.0009, 0.00045, 0.003, 1.3, 3.5, 3.0, 0.5, 0.05, 0.12),
+         (0.0011, 0.00055, 0.0, 1.9, 5.0, 2.0, 0.5, 0.05, 0.08), (0.001, 0.0005, 0.01, 1.5, 3.0, 4.0, 0.8, 0.05, 0.1)]
+T_DMA, DBW = 2.0, 300.0
+LOOK, SEED, TRIES = 0.25, 1, 200
+POLISH, STEPS, HEAT = (0, 1, 4), 25000, 0.0007
 
 
-def build(T, topo, core, rank):
+def build(T, topo, core, rank, costs=None):
+    CY, PCY, PF, GA, SCA, T_HOP, T_RISS, VF, _ = costs or COSTS[0]
     ops = []
 
     def sb(name, a=0, b=None, step=None):
@@ -85,6 +99,9 @@ def build(T, topo, core, rank):
     def v3(name, a, b, h=None):
         t = T[name][:, a // 32:b // 32, :] if h is None else T[name][:, a // 32:b // 32, 16 * h:16 * h + 16]
         return (t, (name, a, b), (b - a) // (1 if h is None else 2))
+
+    def blk(name, k, a, b):
+        return (T[name][:, k, a:b], (name, 32 * k + a, 32 * k + b), b - a)
 
     def ind(win, off):
         return (win[0].indirect(off[0]), [win[1], off[1]], 16 * off[2], "ind")
@@ -115,7 +132,7 @@ def build(T, topo, core, rank):
     def vcost(out, first, k):
         if len(out) == 4: return 0.05 + out[2] * SCA * CY
         if len(first) == 4: return 0.05 + first[2] * GA * CY
-        return 0.05 + max(64, first[2] * k) * CY
+        return VF + max(64, first[2] * k) * CY
 
     def cp(out, a):
         return add("V", lambda g: g.vector.tensor_copy(out[0], a[0]), [out], [a], vcost(out, a, 0.5 if two(out, a) else 1))
@@ -133,28 +150,42 @@ def build(T, topo, core, rank):
         return add("V", lambda g: g.vector.tensor_tensor_scan(out[0], a[0], b[0], 0.0, o0, o1), [out], [a, b],
                    vcost(out, a, 0.5 if two(out, a, b) else 1))
 
-    def red(out, a):
-        return add("V", lambda g: g.vector.tensor_reduce(out[0], a[0], AxisListType.X, A.add), [out], [a], vcost(out, a, 1))
-
     def tr(out, a):
         return add("V", lambda g: g.vector.transpose(out[0], a[0]), [out], [a], vcost(out, a, 1))
 
-    def act(out, a, f, bias=0.0, scale=1.0, acc=None):
-        if acc is None: fn = lambda g: g.scalar.activation(out[0], a[0], f, bias=val(bias), scale=val(scale))
-        else: fn = lambda g: g.scalar.activation(out[0], a[0], f, bias=val(bias), scale=val(scale), accum_out=acc[0])
-        cost = 0.065 + (a[2] * GA if len(a) == 4 else max(64, a[2])) * CY
-        return add("S", fn, [out] + ([acc] if acc else []), [a, bias, scale], cost)
+    def act(out, a, f, bias=0.0, scale=1.0):
+        fn = lambda g: g.scalar.activation(out[0], a[0], f, bias=val(bias), scale=val(scale))
+        cost = 0.065 + a[2] * GA * CY if len(a) == 4 else VF + max(64, a[2]) * CY
+        return add("S", fn, [out], [a, bias, scale], cost)
 
-    def mm(out, l, r, grp, first=False):
-        k = 4 if SCRATCH[l[1][0]][2] == "float32" else 1
-        d = add("P", None, [out], [l, r], 0.02 + max(64, r[2]) * k * PCY, grp=grp, acc=not first)
-        d["mm"] = (out[0], l[0], r[0], first)
+    def mms(items, grp=None):
+        cost = sum(PF + max(min(64, l[2]), r[2]) * (4 if SCRATCH[l[1][0]][2] == "float32" else 1) * PCY for _, l, r, _, _ in items)
+        d = add("P", None, [i[0] for i in items], [x for i in items for x in i[1:3]], cost, grp=grp or len(ops), acc=not items[0][3])
+        d["mm"] = [(o[0], l[0], r[0], a, b) for o, l, r, a, b in items]
+        d["shared"] = grp is not None
         return d
 
-    def iota(out, pat, base, cm):
+    def total(terms):
+        return [t + (k == 0, k == len(terms) - 1) for k, t in enumerate(terms)]
+
+    def apart(terms, grp, first=False):
+        d = mms([t + (True, True) for t in terms], grp)
+        d["shared"], d["acc"] = False, not first
+
+    def more(terms, grp, first=False):
+        return mms([t + (first and k == 0, False) for k, t in enumerate(terms)], grp)
+
+    def iota(out, pat, base, cm=0):
         if SCRATCH[out[1][0]][2] == "int32": fn = lambda g: g.iota(out[0], pat, base, cm)
         else: fn = lambda g: g.iota(out[0], pat, base, cm, allow_small_or_imprecise_dtypes=True)
         return add("G", fn, [out], [], 0.13 + 2 * out[2] * CY)
+
+    def fill(out, c):
+        return iota(out, [[0, out[2]]], c)
+
+    def select(out, a, op, pat, base, cm):
+        fn = lambda g: g.affine_select(out[0], a[0], pat, op, 0.0, base, cm)
+        return add("G", fn, [out], [a], 0.17 + 2 * a[2] * CY)
 
     nl = [0]
 
@@ -165,278 +196,323 @@ def build(T, topo, core, rank):
         outs = [out] if isinstance(out, tuple) else []
         return add(q, fn, outs, [a], 0.06, lat=T_DMA + kb / DBW, tok=(s, 16))
 
-    def send(src, dests, kb):
-        for k, land, m in dests:
-            c = T.cores[(rank + k) % len(T.cores)]
-            back = T.cores[(rank - k) % len(T.cores)]
+    def share(a, b, k, n):
+        parts = [topo.engines(a, b)]
+        while len(parts) < n:
+            i = max(range(len(parts)), key=lambda i: (len(parts[i]), i))
+            e = parts.pop(i)
+            parts[i:i] = [e[:len(e) // 2], e[len(e) // 2:]]
+        return parts[k]
+
+    def send(items):
+        n, trs, cnt = len(items), [], 0
+        for k, (src, ahead, land, m) in enumerate(items):
+            c = T.cores[(rank + ahead) % len(T.cores)]
             rid, pid, _ = topo.addr(c)
-            fn = (lambda land, m, rid, pid, mk: lambda g: g.remote_dma(land[0], src[0], T.sem["r_" + m], T.sem.sent, pid, rid, mk))(
-                land, m, rid, pid, topo.mask(core, c))
-            s = add("G", fn, [], [src], T_RISS, tok="none", sent=len(topo.engines(core, c)))
-            r = add("R", None, [land], [], 0.0, lat=T_HOP + kb / 80.0, tok=("r_" + m, len(topo.engines(back, core))))
-            r["after"] = s["id"]
+            eng = share(core, c, k, n)
+            cnt += len(eng)
+            trs.append((land[0], src[0], T.sem["r_" + m], pid, rid, sum(1 << e for e in eng)))
+        if n == 1:
+            d, s, sem, pid, rid, mk = trs[0]
+            fn = lambda g: g.remote_dma(d, s, sem, T.sem.sent, pid, rid, mk)
+        else:
+            fn = lambda g: g.remote_dma_fused([RemoteDMATransfer(dst_ids=[DstId(rid=rid, pnc=pid)], dma_engine_mask=mk, remote_sem=sem,
+                                                                 src=s, dst=d) for d, s, sem, pid, rid, mk in trs], local_sem=T.sem.sent)
+        call = add("G", fn, [], [i[0] for i in items], T_RISS, tok="none", sent=cnt)
+        for k, (src, ahead, land, m) in enumerate(items):
+            back = T.cores[(rank - ahead) % len(T.cores)]
+            r = add("R", None, [land], [], 0.0, lat=T_HOP + n * src[2] / 320.0, tok=("r_" + m, len(share(back, core, k, n))))
+            r["after"] = call["id"]
 
     col = lambda k: sb("cf", k, k + 1)
     E = lambda name, i: sb(name, 15 - i, 143 - i)
+    D = lambda k: sb("dg", 128 * k, 128 * k + 128)
+    gi = sb("bo", 0, 128, 16)
+    idb, idn, i16, i64, i2k, i65 = sb("idb"), D(0), D(1), D(2), D(3), D(4)
+    idf, nidf = [sb("df", 128 * k, 128 * k + 128) for k in range(2)]
+    bo, nbo, lo, up = [sb("bo", 128 * k, 128 * k + 128) for k in range(4)]
 
     dma("Y", sb("mi"), T.mem0[:], 128)
     dma("S", sb("ei"), T.inv0[:], 128)
     dma("Y", sb("xw", 0, 2048), T.xs[:, 0:2048], 700)
     dma("S", sb("xw", 2048, 4096), T.xs[:, 2048:4096], 1000)
     iota(sb("pi"), [[0, 1]], 0, 1)
-    iota(sb("jf"), [[1, 160]], 0, 0)
-    for k, m in enumerate((15, 112, 96, 16, 1, 12, 2, 7)):
+    iota(sb("jf"), [[1, 160]], 0)
+    for k, m in enumerate((15, 112, 96, 16)):
         ts(sb("ci", k, k + 1), sb("pi"), m, A.bitwise_and)
-    cp(sb("cf", 0, 6), sb("ci", 0, 6))
-    cp(sb("cf", 28, 30), sb("ci", 6, 8))
+    cp(sb("cf", 0, 4), sb("ci", 0, 4))
     ts(col(6), col(2), col(0), A.subtract, 31.0, A.add)
     ts(col(7), col(3), 0.0, A.is_equal)
     ts(col(8), col(3), 0.0, A.is_gt)
     for e in range(2):
         ts(sb("rr", 144 * e, 144 * e + 144), sb("jf", 0, 144), col(6), A.is_equal, col(7 + e), A.mult)
-    ts(col(30), col(0), 2.0, A.mult, 15.0, A.add)
-    ts(col(9), col(29), 30.0, A.mult, col(30), A.add)
-    ts(sb("ol", 0, 16), sb("jf", 0, 16), -1.0, A.mult, col(9), A.add)
-    ts(col(31), col(28), 8.0, A.mult, 15.0, A.add)
-    ts(col(10), col(4), 32.0, A.mult, col(31), A.add)
-    ts(col(11), col(5), -0.25, A.mult, col(10), A.add)
-    ts(sb("ol", 16, 20), sb("jf", 0, 4), -4.0, A.mult, col(11), A.add)
-    cp(sb("ol", 20, 21), col(10))
-    iota(sb("jx"), [[64, 2], [16, 2], [32, 2]], 15, 0)
-    cp(sb("ol", 24, 32), sb("jx"))
+    act(sb("rb"), sb("rr"), F.Copy)
     ts(sb("b1"), sb("jf", 0, 144), col(1), A.subtract, 15.0, A.is_equal)
-    act(sb("b8"), sb("b1"), F.Copy, scale=BIG)
-    act(sb("b4"), sb("b1"), F.Copy, scale=BIG / 2)
+    act(sb("b2"), sb("b1"), F.Copy, scale=2.0)
     act(sb("bf"), sb("b1"), F.Copy)
-    tt(sb("ea"), E("bf", 0), E("bf", 1), A.subtract)
-    cp(col(12), sb("pi"))
-    ts(sb("idb"), sb("jf", 0, 128), col(12), A.is_equal)
-    act(sb("idn"), sb("idb"), F.Copy, scale=-1.0)
-    act(sb("idf"), sb("idb"), F.Copy)
-    iota(sb("xw", 4096, XW), [[0, XW - 4096]], 0, 0)
-    iota(sb("zero"), [[0, 128]], 0, 0)
-    iota(sb("ones"), [[0, 448]], 1, 0)
-    iota(sb("jg"), [[16, 8], [0, 16]], 0, 0)
-    iota(sb("jc"), [[0, 4], [1, 16]], 0, 0)
-    ts(sb("bo"), sb("jg"), col(1), A.is_equal)
-    ts(sb("cf", 16, 20), sb("jf", 0, 64, 16), col(0), A.add, 0.5, A.add)
-    dr = {}
-    for k, r in enumerate(sorted(set(ROWS.values()) - {0})):
-        dr[r] = sb("dr", 128 * k, 128 * k + 128)
-        ts(col(24 + k), col(0), float(r), A.is_lt, 8 * BIG, A.mult)
-        act(dr[r], sb("idb"), F.Copy, scale=col(24 + k))
-    ts(col(14), col(0), 15.0, A.is_equal)
-    ts(sb("fake"), sb("jf", 0, 64), V + 1.0, A.add, col(14), A.mult)
-    ts(sb("pm", 0, 64), sb("jc"), col(0), A.is_equal)
-    act(sb("pm", 64, 128), sb("pm", 0, 64), F.Copy, scale=-1.0)
-    wb, db = {}, {}
+    fill(sb("ea"), 0)
+    for k in range(2):
+        act(sb("ea", k, 128, 16), sb("b1", 15, 143, 16), F.Copy, scale=1.0 - 2 * k)
+    fill(sb("ones", 0, 160), 1)
+    fill(sb("ones", 160, 448), 1)
+    select(idb, sb("ones", 0, 128), A.is_equal, [[-1, 128]], 0, 1)
+    for k, s in enumerate((-1.0, 16.0, KS, -V / 2.0, -16.0 * V)):
+        act(D(k), idb, F.Copy, scale=s)
+    for k, s in enumerate((1.0, -1.0)):
+        act(sb("df", 128 * k, 128 * k + 128), idb, F.Copy, scale=s)
+    r0 = 16 * OL_NEW
+    iota(sb("row", 0, 256), [[-1, 16], [16, 2], [32, 8]], 14)
+    iota(sb("row", 256, 288), [[0, 2], [16, 2], [32, 8]], 15)
+    iota(sb("row", r0, r0 + 8), [[0, 2], [16, 2], [32, 2]], 128 + 15)
+    iota(sb("row", r0 + 8, r0 + 64), [[-1, 14], [16, 2], [32, 2]], 13)
+    iota(sb("row", r0 + 64, r0 + 96), [[0, 8], [16, 2], [32, 2]], 192 + 15)
+    iota(sb("row", 16 * OL_VS, 16 * OL_VS + VS), [[-1, 16], [16, 2], [32, VS // 32]], 15)
+    if 16 * OL_X > 16 * OL_VS + VS: fill(sb("row", 16 * OL_VS + VS, 16 * OL_X), 0)
+    iota(sb("row", 16 * OL_X, 16 * OL_X + 64), [[1, 2], [2, 2], [0, 16]], 0)
+    for a, b, ps in ((0, OL_NEW, "px"), (OL_NEW, OLW, "pd2")):
+        mms(total([(sb(ps, a, b), E("b1", c), sb("row", 16 * a + c, 16 * b, 16)) for c in range(16)]))
+        ts(sb("ol", a, b), sb(ps, a, b), 1.0 / 16, A.mult)
+    act(sb("xw", V, XW), sb("ones", 0, XW - V), F.Copy, scale=-2.0 ** 99)
+    act(sb("xw", V, XW), sb("xw", V, XW), F.Copy, scale=4.0)
+    iota(sb("jc"), [[0, 4], [1, 16]], 0)
+    select(lo, sb("ones", 0, 128), A.is_ge, [[-16, 8], [0, 16]], 0, 1)
+    select(bo, lo, A.is_ge, [[16, 8], [0, 16]], 15, -1)
+    act(nbo, bo, F.Copy, scale=-KS)
+    select(lo, bo, A.is_ge, [[1, 128]], 0, -1)
+    select(up, bo, A.is_gt, [[-1, 128]], 0, 1)
+    act(sb("jc"), sb("jc"), F.Abs, bias=col(0), scale=-1.0)
+    act(sb("pm"), sb("jc"), F.Relu, bias=1.0, scale=-1.0)
+    fill(sb("fl", 256, 256 + 3 * 136), 0)
+    fill(sb("cst", 0, SS), 16)
+    fill(sb("cst", SS, S0), 0)
+    fill(sb("cst", S0, 448), 16)
+    fill(sb("neg"), -1)
+    fill(sb("thr"), 0)
+    act(col(11), col(0), F.Identity, bias=KS / 2, scale=KS)
+    act(sb("thr", 0, 128, 32), sb("jf", 0, 4), F.Identity, bias=col(11), scale=16 * KS)
+    iota(sb("seg"), [[0, 4], [1, 32]], 0)
+    select(sb("rst"), sb("ones", 0, 160), A.is_gt, [[0, 5], [1, 32]], 0, 0)
+    fill(sb("hw", 0, 8), 0)
+    fill(sb("hw", 8, 40), 1)
     for t in range(NT):
-        if TB[t] not in wb:
-            wb[TB[t]] = col(20 + t)
-            ts(col(20 + t), col(0), 0.0, A.is_gt, BIG * TB[t], A.mult)
-        if TA[t] not in db:
-            db[TA[t]] = sb("dg", 128 * t, 128 * t + 128)
-            act(db[TA[t]], sb("idb"), F.Copy, scale=BIG * (1 - TA[t]))
-        n = S0 + C * t
-        for nm, c in (("mw", 0), ("ew", 0), ("ww", 0), ("hb", 1)):
-            iota(sb(nm, 512 * t + n, 512 * t + n + 64), [[0, 64]], c, 0)
+        n = 512 * t + S0 + C * t
+        iota(sb("mw", n, n + 64), [[1, 64]], V + 1 - int(OFF))
+        for nm, c in (("ew", 0), ("ww", 0), ("sg", -1)):
+            fill(sb(nm, n, n + 64), c)
     for k in range(8):
-        iota(sb("ft", k * (XW // 8), (k + 1) * (XW // 8)), [[0, XW // 8]], 0, 0)
+        fill(sb("ft", k * (XW // 8), (k + 1) * (XW // 8)), 0)
 
-    def arrange(ps, w, half, grp):
-        for e in range(2):
-            for h in range(2):
-                mm(v3(ps, 0, w, e), sb("rr", 144 * e + 16 - 16 * h, 144 * e + 144 - 16 * h), half(h), grp + (e,), h == 0)
+    def arrange(ps, c0, w, half, one, plus=None):
+        side = [[(v3(ps, c0, c0 + w, e), sb(rr, 144 * e + 16 - 16 * h, 144 * e + 144 - 16 * h), f(h))
+                 for rr, f in (("rr", half), ("rb", plus)) if f for h in range(2)] for e in range(2)]
+        if one: mms(total([(v3(ps, c0, c0 + w), idb, sb("ones", 0, w))] + side[0] + side[1]))
+        else: mms(total(side[0]) + total(side[1]))
 
-    ts(sb("mw", 0, 256), sb("mi"), -1.0, A.mult, float(V), A.add)
-    arrange("pd2", 256, lambda h: sb("mw", 128 * h, 128 * h + 128), ("sm",))
-    tr(sb("tp", 0, 256), v3("pd2", 0, 256))
-    act(sb("nz"), sb("tp", 0, 256), F.Relu, bias=1.0, scale=-1.0)
-    scan(sb("sc"), sb("nz"), sb("tp", 0, 256), A.mult, A.add)
-    ts(sb("ts0", 512, 528), ind(sb("sc"), sb("ol", 0, 1)), -1.0, A.mult, float(V), A.add)
-    ts(sb("ts0", 0, 256), ind(sb("tp", 0, 256), sb("ol", 0, 16)), -1.0, A.mult, float(V), A.add)
-    ts(sb("ein", 0, 256), sb("ei"), -1.0, A.mult, float(V), A.add)
-    arrange("pd3", 256, lambda h: sb("ein", 128 * h, 128 * h + 128), ("se",))
-    tr(sb("tp", 256, 512), v3("pd3", 0, 256))
-    ts(sb("ts0", 256, 512), ind(sb("tp", 256, 512), sb("ol", 0, 16)), -1.0, A.mult, float(V), A.add)
-    send(sb("ts0", 16, TSW), [(k, sb("uin", U_TS[k] + 16, U_TS[k] + TSW), "ts%d" % k) for k in (1, 2, 3)], 128)
+    u0 = U_TS[0]
+    ts(sb("t0", 0, 256), sb("mi"), V - 1.0, A.min, OFF, A.subtract)
+    ts(sb("fl", 0, 256), sb("mi"), float(V), A.is_equal, OFF - V + 1, A.mult)
+    tt(sb("mw", 0, 256), sb("t0", 0, 256), sb("fl", 0, 256), A.add)
+    arrange("pm1", 0, 256, lambda h: sb("t0", 128 * h, 128 * h + 128), True, lambda h: sb("fl", 128 * h, 128 * h + 128))
+    tr(sb("t0", 256, 512), v3("pm1", 0, 256))
+    scan(sb("t0", 512, 768), sb("t0", 256, 512), sb("t0", 256, 512), A.mult, A.min)
+    ts(sb("uin", u0, u0 + 16), ind(sb("t0", 512, 768), sb("ol", 16, 17)), OFF - 1, A.add, XW - 1.0, A.min)
+    ts(sb("uin", u0 + 16, u0 + 272), ind(sb("t0", 256, 512), sb("ol", 0, 16)), OFF - 1, A.add, XW - 1.0, A.min)
+    ts(sb("ew", 0, 256), sb("ei"), float(V), A.subtract)
+    cp(sb("uin", u0 + 256 + VS, u0 + TSW), sb("ei"))
+    cp(sb("eh", 0, 256), sb("ei"))
+    arrange("pm1", 256, VS, lambda h: sb("ew", SS + VS // 2 * h, SS + VS // 2 * (h + 1)), False)
+    tr(sb("t0", 768, 768 + VS), v3("pm1", 256, 256 + VS))
+    ts(sb("uin", u0 + 256, u0 + 256 + VS), ind(sb("t0", 768, 768 + VS), sb("ol", OL_VS, OL_VS + VS // 16)), float(V), A.add)
+    for k in (1, 2, 3):
+        send([(sb("uin", u0, u0 + TSW), k, sb("uin", U_TS[k], U_TS[k] + TSW), "ts%d" % k)])
 
     xwin = sb("xw", 0, XW)
-    bank = [0, 0]
+    bank = [0]
 
-    def compare(t, j, part):
-        par = t % 2
+    def members(t, j):
+        pm, x0, cb = "pm%d" % (t % 2), XL * t, CW * (t % 2)
         if j is None:
-            nm, u, w, c0, x0, rep = ("ts0", 0, 256, 0, 0, 2) if t == 0 else ("uin", U_TS[t], 256, 0, 0, 2)
-            um, ue, ul, lw = u, u + 256, u + 512, 16
+            u, w, c0, first = U_TS[t], 256, 0, 1
+            xe = x0 + 768
+            act(sb("xl", xe - 256, xe), ind(xwin, sb("uin", u, u + 16)), F.Copy)
+            for k in range(1, max(M_RUNS[t])):
+                dma("Y", sb("xl", xe - 256 * (k + 1), xe - 256 * k), sb("xl", xe - 256, xe), 64)
+            for k in range(3 if ON_V[t] else 0):
+                dma("Y", sb("xl", xe + VS * k, xe + VS * (k + 1)), sb("xl", xe - VS, xe), 24)
+            runs = M_RUNS[t]
         else:
-            nm, u, w, c0, x0, rep = "uin", U_NEW[(t, j)], 64, S0 + C * j, 512 + 256 * j, 4
-            um, ue, ul, lw = u, u + 80, u + 64, 16
-        k = w // 16
-        x0 += 1280 * t
-        cb = CW * par + 31 * c0
-        if part == "m":
-            act(sb("xl", x0, x0 + 256), ind(xwin, sb(nm, ul, ul + lw)), F.Copy)
-            if j is None: act(sb("xl", x0 + 256, x0 + 512), sb("xl", x0, x0 + 256), F.Copy)
-            i = 1
-            while i < 16:
-                i2 = min(16, (i // rep + 1) * rep)
-                o = cb + (i - 1) * w
-                tt(sb("cmp", o, o + (i2 - i) * w), ind(xwin, sb(nm, um + k * i, um + k * i2)), sb("xl", x0, x0 + (i2 - i) * w), A.is_equal)
-                for r in range(i, i2):
-                    mm(v3("pm%d" % par, c0, c0 + w), E("b1", r), sb("cmp", cb + (r - 1) * w, cb + r * w), ("m", t))
-                i = i2
-            return
-        cb += 15 * w
-        i = 0
-        newest = j is not None and j == t - 1
-        R0 = ROWS[(t, j)]
-        if R0: mm(v3("pe%d" % par, c0, c0 + w), dr[R0], sb("ones", 0, w), ("e", t))
-        while i < R0:
-            i2 = min(R0, i + 512 // w)
-            ln = (i2 - i) * w
-            xo = 16 * 448 * par + 16 * c0 + i * w
-            act(sb("xe", xo, xo + ln), ind(xwin, sb(nm, ue + k * i, ue + k * i2)), F.Copy)
-            b = 1 if newest else 0
-            pd = "pd%d" % (2 * b + bank[b] % 2); bank[b] += 1
-            grp = ("d", t, j, i)
-            mm(v3(pd, 0, ln), sb("idb"), sb("xe", xo, xo + ln), grp, True)
-            for o in range(0, ln, rep * w):
-                o2 = min(ln, o + rep * w)
-                mm(v3(pd, o, o2), sb("idn"), sb("xl", x0, x0 + o2 - o), grp)
-            act(sb("cmp", cb + i * w, cb + i2 * w), v3(pd, 0, ln), F.Sign, bias=EPS)
-            for r in range(i, i2):
-                mm(v3("pe%d" % par, c0, c0 + w), E("b4", r), sb("cmp", cb + r * w, cb + (r + 1) * w), ("e", t))
-            i = i2
-        while i < 16:
-            i2 = min(16, i + rep)
-            tt(sb("cmp", cb + i * w, cb + i2 * w), ind(xwin, sb(nm, ue + k * i, ue + k * i2)), sb("xl", x0, x0 + (i2 - i) * w), A.is_ge)
-            for r in range(i, i2):
-                mm(v3("pe%d" % par, c0, c0 + w), E("b8", r), sb("cmp", cb + r * w, cb + (r + 1) * w), ("e", t))
-            i = i2
+            u, w, c0, first = U_A[(t, j)], 64, S0 + C * j, 2
+            xe = x0 + 768 + 3 * VS + 512 * (j + 1)
+            cb += 15 * 256 + 14 * 64 * j
+            act(sb("xl", xe - 128, xe), ind(xwin, sb("uin", u, u + 8)), F.Copy)
+            runs = (2,) * 7 if j == t - 1 else OLD_RUNS
+            for k in range(1, max(runs) // 2):
+                dma("Y", sb("xl", xe - 128 * (k + 1), xe - 128 * k), sb("xl", xe - 128, xe), 32)
+        if j is None: cell = lambda i, h: (T[pm][:, 4 * h:4 * h + 4, i:32:16], (pm, 0, 256), 8)
+        elif j < t - 1: cell = lambda i, h: (T[pm][:, c0 // 32:c0 // 32 + 2, i // 2:32:8], (pm, c0, c0 + 64), 8)
+        else: cell = lambda i, h: sb("px", i // 2, 64, 8)
+        grp = ("m", t, j == t - 1)
+        apart([(cell(0, h), sb("ones", 0, 128), gi) for h in range(2 if j is None else 1)], grp, j is None or j == t - 1)
+        k, i = w // 16, first
+        for nr in runs:
+            o, ln = cb + (i - first) * w, nr * w
+            tt(sb("cmp", o, o + ln), ind(xwin, sb("uin", u + k * i, u + k * (i + nr))), sb("xl", xe - ln, xe), A.is_equal)
+            apart([(cell(i + 128 * q // w, q % 2), sb("cmp", o + 128 * q, o + 128 * (q + 1)), gi) for q in range(ln // 128)], grp)
+            i += nr
+
+    def enough(t, js):
+        pm, back = "pm%d" % (t % 2), []
+        for j in js:
+            if j is None:
+                act(sb("fl", 0, 256), v3(pm, 0, 256), F.Relu, bias=1.0 - TB[t])
+                for h in range(2):
+                    back += total([(v3(pm, 128 * h, 128 * h + 128), sb("fl", 128 * h, 128 * h + 128), i65)])
+            else:
+                f, c0 = 256 + 136 * (j if j < t - 1 else 2), S0 + C * j
+                act(sb("fl", f + 1, f + 129, 2), v3(pm, c0, c0 + 64) if j < t - 1 else sb("px", 0, 64), F.Relu, bias=1.0 - TB[t])
+                back += total([(v3(pm, c0, c0 + 64), sb("fl", f + 1 - h, f + 129 - h), sb("dg", 512 + 64 * h, 576 + 64 * h)) for h in range(2)])
+        mms(back)
+
+    def bounds(t, j):
+        par = t % 2
+        pe, cb = "pe%d" % par, CW * par + 15 * 256 + 14 * 192
+        if j is None:
+            u, xv = U_TS[t] + 256, XL * t + 768 - VS
+            for i in range(0, 16 if ON_V[t] else 0, 4):
+                o = cb + 16 * SS + i * VS
+                tt(sb("cmp", o, o + 4 * VS), ind(xwin, sb("uin", u + VS // 16 * i, u + VS // 16 * (i + 4))), sb("xl", xv, xv + 4 * VS), A.is_ge)
+                more([(sb(pe, SS, S0), E("b2", i + r), sb("cmp", o + r * VS, o + (r + 1) * VS)) for r in range(4)], ("e", t, False))
+            parts, c0 = [], 0
+            for w, step, rows in S_PARTS + ([] if ON_V[t] else [V_PART]):
+                parts.append((c0, w, XL * t + 512 + c0, 1, step, rows))
+                c0 += w
+        else:
+            parts = [(S0 + C * j, 64, XL * t + 768 + 3 * VS + 512 * (j + 1) - 128, 2, 32 if j == t - 1 else OLD_GATHER, (8, 8))]
+        for c0, w, x0, rep, step, rows in parts:
+            u, xo, o = U_TS[t] + 256 + VS + c0, XE * par + 16 * c0, cb + 16 * c0
+            for s in range(0, w, step):
+                out, got = sb("xe", xo + 16 * s, xo + 16 * (s + step)), ind(xwin, sb("uin", u + s, u + s + step))
+                if (t, j, s // step) in V_GATHERS: cp(out, got)
+                else: act(out, got, F.Copy)
+            i = 0
+            for k, nr in enumerate(rows):
+                if j is not None and j == t - 1: pd = ("pd2", "px")[k]
+                else:
+                    pd = "pd%d" % (bank[0] % 2); bank[0] += 1
+                run = []
+                for r in range(0, nr, rep):
+                    run += total([(sb(pd, r * w, (r + rep) * w), idn, sb("xl", x0, x0 + rep * w))] +
+                                 [(sb(pd, q * w, (q + 1) * w), idb, sb("xe", xo + i + q, xo + 16 * w, 16)) for q in range(r, r + rep)])
+                mms(run)
+                if (t, j, k) in V_SIGNS: ts(sb("cmp", o + i * w, o + (i + nr) * w), sb(pd, 0, nr * w), 0.0, A.is_ge, 0.5, A.subtract)
+                else: act(sb("cmp", o + i * w, o + (i + nr) * w), sb(pd, 0, nr * w), F.Sign, bias=EPS)
+                e = "b2" if (t, j, k) in V_SIGNS else "b1"
+                new = j == t - 1
+                more([(sb("pd2", 0, w) if new else sb(pe, c0, c0 + w), E(e, r), sb("cmp", o + r * w, o + (r + 1) * w))
+                      for r in range(i, i + nr)], ("e", t, new), new and k == 0)
+                i += nr
 
     def early(t):
-        n, par = S0 + C * t, t % 2
-        mm(v3("pm%d" % par, 0, n), sb("zero"), sb("ones", 0, n), ("m", t), True)
-        mm(v3("pe%d" % par, 0, n), db[TA[t]], sb("ones", 0, n), ("e", t), True)
+        n, par = S0 + C * max(0, t - 1), t % 2
+        more([(sb("pe%d" % par, 0, n), idb, sb("cst", 0, n)) if ON_V[t] else (sb("pe%d" % par, 0, n), i16, sb("ones", 0, n))],
+             ("e", t, False), True)
         for j in [None] + list(range(t - 1)):
-            compare(t, j, "m")
-            compare(t, j, "e")
+            members(t, j)
+            bounds(t, j)
+        enough(t, [None] + list(range(t - 1)))
 
     def decide(t):
         n, par, b = S0 + C * t, t % 2, 512 * t
         N = n + 64
         pm, pe = "pm%d" % par, "pe%d" % par
-        gs = lambda k: sb("gs", 64 * k, 64 * k + 64) if k != 2 else sb("gs", 64 * (2, 7, 8, 9)[t], 64 * (2, 7, 8, 9)[t] + 64)
-        ns, i0, lt, hv = IDS_S[t], 8 * t, sb("lt", 16 * t, 16 * t + 4), sb("hv", 64 + 64 * t, 128 + 64 * t)
-        iv = sb("inv", 512 * par, 512 * par + n)
-        if t == 0:
-            act(iv, sb("mw", 0, 256), F.Relu, bias=16.0, scale=-16.0)
-        else:
-            cp(sb("mw", b, b + n), sb("uin", U_M[t], U_M[t] + n))
-            if ON_S["inv"]: act(iv, sb("mw", b, b + n), F.Relu, bias=16.0, scale=-16.0)
-            else: ts(iv, sb("uin", U_M[t], U_M[t] + n), 0.0, A.is_equal, 16.0, A.mult)
-            compare(t, t - 1, "m")
-            cp(sb("ein", b, b + n - 64), sb("uin", U_E[t], U_E[t] + n - 64))
-            u = U_NEW[(t, t - 1)]
-            cp(sb("ein", b + n - 64, b + n), sb("uin", u + 144, u + 208))
-            compare(t, t - 1, "e")
-        mm(v3(pm, 0, n), sb("idb"), iv, ("m", t))
-        act(sb("ww", b, b + n), v3(pm, 0, n), F.Relu, bias=wb[TB[t]], scale=-BIG)
-        mm(v3(pm, 0, n), sb("bo"), sb("ww", b, b + n), ("h", t), True)
-        act(sb("hb", b, b + n), v3(pm, 0, n), F.Sign)
-        scan(sb("cum", 0, N), sb("hb", b, b + N), sb("hb", b, b + N), A.add, A.max)
-        for d in range(4):
-            jk = sb("junk", 512 * d, 512 * d + N)
-            if d < ns:
-                act(jk, sb("cum", 0, N), F.Sign, bias=col(16 + d), scale=-1.0, acc=sb("acc", d, d + 1))
-            else:
-                ts(jk, sb("cum", 0, N), col(16 + d), A.is_le)
-                red(sb("acc", d, d + 1), jk)
-        if ns < 4: cp(sb("ids", i0 + ns, i0 + 4), sb("acc", ns, 4))
-        if ns > 0: ts(sb("ids", i0, i0 + ns), sb("acc", 0, ns), float(N), A.add, 0.5, A.mult)
-        ids = sb("ids", i0, i0 + 4)
-        mwin, ewin, wwin = sb("mw", b, b + N), sb("ew", b, b + N), sb("ww", b, b + N)
-        go, mfk = (T.g1[:, 0], ("g1", 0, 64), 64), (T.g1[:, 1], ("g1", 64, 128), 64)
-        if ON_S["gw"]: act(gs(0), ind(wwin, ids), F.Copy)
-        else: cp(gs(0), ind(wwin, ids))
-        tt(go, ind(mwin, ids), gs(0), A.min)
-        tt(mfk, ind(mwin, ids), sb("fake"), A.max)
-        act(gs(1), ind(mwin, ids), F.Copy)
-        arrange(pm, 128, lambda h: (T.g1[:, :, 32 * h:32 * h + 32], ("g1", 0, 128), 64), ("a1", t))
-        tr(sb("tp", 512, 640), v3(pm, 0, 128))
-        if ON_S["nz"]: act(sb("nz", 0, 128), sb("tp", 512, 640), F.Relu, bias=1.0, scale=-1.0)
-        else: ts(sb("nz", 0, 128), sb("tp", 512, 640), 0.0, A.is_equal)
-        scan(sb("sc", 0, 128), sb("nz", 0, 128), sb("tp", 512, 640), A.mult, A.add)
-        o = O_NEW[t]
-        if t < 3:
-            ts(sb("uout", o, o + 64), ind(sb("tp", 512, 576), sb("ol", 16, 20)), -1.0, A.mult, float(V), A.add)
-            ts(sb("uout", o + 64, o + 80), ind(sb("sc", 0, 64), sb("ol", 20, 21)), -1.0, A.mult, float(V), A.add)
-            u = U_NEW[(t + 1, t)]
-            send(sb("uout", o + 4, o + 80), [(1, sb("uin", u + 4, u + 80), "a%d" % t)], 19)
-        tt(gs(2), gs(1), go, A.subtract)
-        cp(ind(mwin, ids), gs(2))
-        cp(sb("uout", O_M[t], O_M[t] + n), sb("mw", b, b + n))
-        cp(sb("uout", O_M[t] + n, O_M[t] + N), go)
-        send(sb("uout", O_M[t], O_M[t] + N), [(1, sb("uin", U_M[t + 1], U_M[t + 1] + N), "b%d" % t)], N / 4)
-        tt(sb("xx"), ind(sb("sc", 0, 128), sb("ol", 24, 32)), sb("pm"), A.mult)
-        cp(sb("lt", 16 * t, 16 * t + 16), ind(sb("sc", 64, 128), sb("ol", 20, 21)))
-        mm(v3(pm, 128, 192), sb("ea"), sb("xx", 0, 64), ("ta", t), True)
-        mm(v3(pm, 128, 192), sb("ea"), sb("xx", 64, 128), ("ta", t))
-        mm(v3(pm, 192, 256), E("bf", 1), sb("xx", 0, 64), ("tb", t), True)
-        mm(v3(pm, 192, 256), E("bf", 1), sb("xx", 64, 128), ("tb", t))
-        if ON_S["hv"]: act(sb("hv", 0, 64), v3(pm, 128, 192), F.Copy)
-        else: cp(sb("hv", 0, 64), v3(pm, 128, 192))
-        tt(hv, sb("hv", 0, 64), v3(pm, 192, 256), A.add)
-        cp(ind(sb("ft"), lt), hv)
-        tt(sb("ew", b, b + n), sb("ein", b, b + n), v3(pe, 0, n), A.min)
-        cp(sb("uout", O_E[t], O_E[t] + n), sb("ew", b, b + n))
-        send(sb("uout", O_E[t], O_E[t] + n), [(1, sb("uin", U_E[t + 1], U_E[t + 1] + n), "c%d" % t)], n / 4)
-        act(gs(3), ind(ewin, ids), F.Relu)
-        if ON_S["dead"]: act(gs(4), ind(ewin, ids), F.Relu, bias=BIG, scale=-BIG)
-        else: ts(gs(4), ind(ewin, ids), 0.0, A.is_le, BIG, A.mult)
-        tt(gs(5), gs(4), gs(2), A.min)
-        if t < 3:
-            tt(sb("g2"), gs(3), gs(5), A.subtract)
-            arrange("pd2", 64, lambda h: sb("g2", 32 * h, 32 * h + 32), ("a2", t))
-            tr(sb("tp", 640, 704), v3("pd2", 0, 64))
-            cp(sb("fo"), ind(sb("tp", 640, 704), sb("ol", 16, 20)))
-            act(gs(6), ind(sb("tp", 640, 704), sb("ol", 16, 20)), F.Abs)
-        else:
-            cp(sb("fo"), ind(ewin, ids))
+        gs = lambda k: sb("gs", 64 * k, 64 * k + 64)
+        ue = U_TS[t] + 256 + VS
+        if t:
+            ts(sb("mw", b, b + n), sb("uin", U_M[t], U_M[t] + n), OFF, A.subtract)
+            members(t, t - 1)
+            enough(t, [t - 1])
+            ts(sb("ew", b, b + n), sb("uin", ue, ue + n), float(V), A.subtract)
+            more([(sb(pe, 0, n - 64), i64, sb("sp", 512 * t, 512 * t + n - 64))], ("e", t, False))
+        tt(sb("ww", b, b + n), v3(pm, 0, n), sb("mw", b, b + n), A.is_gt)
+        mms(total([(blk(pm, 0, 0, n // 16), E("b1", c), sb("ww", b + c, b + n, 16)) for c in range(16)]))
+        act(sb("hw", 8, 8 + n // 16), blk(pm, 0, 0, n // 16), F.Sign)
+        mms(total([(sb("px", 0, 128), idb, sb("thr"))] + [(sb("px", 32 * d + 1, 32 * d + 32), nbo, sb("hw", 8, 39)) for d in range(4)]) +
+            total([(sb("px", 128, 160), lo, sb("hw", 8, 40)), (sb("px", 128, 160), up, sb("hw", 7, 39))]))
+        scan(sb("cs"), sb("rst"), sb("px", 0, 160), A.mult, A.add)
+        if t: bounds(t, t - 1)
+        scan(sb("c2"), sb("cs", 0, 128), sb("seg", 0, 128), A.max, A.min)
+        run, ids = sb("ids", 16 * t, 16 * t + 4), sb("ids", 16 * t + 8, 16 * t + 12)
+        cp(run, sb("c2", 31, 128, 32))
+        tt(sb("fi"), ind(sb("cs", 128, 160), run), sb("jf", 0, 64), A.is_le)
+        mms(total([(blk(pm, 0, 0, 4), i16, sb("c2", 31, 128, 32))] + [(blk(pm, 0, 0, 4), E("b1", c), sb("fi", c, 64, 16)) for c in range(16)]))
+        cp(ids, blk(pm, 0, 0, 4))
+        mwin, ewin, wwin, swin = sb("mw", b, b + N), sb("ew", b, b + N), sb("ww", b, b + N), sb("sg", b, b + N)
+        go, raw = (T.g1[:, 0], ("g1", 0, 64), 64), (T.g1[:, 1], ("g1", 64, 128), 64)
+        act(raw, ind(mwin, ids), F.Copy)
+        tt(go, ind(wwin, ids), raw, A.mult)
+        arrange(pm, 0, 128, lambda h: (T.g1[:, :, 32 * h:32 * h + 32], ("g1", 0, 128), 64), True)
+        tr(sb("tp", 0, 128), v3(pm, 0, 128))
+        scan(sb("tp", 128, 256), sb("tp", 0, 128), sb("tp", 0, 128), A.mult, A.min)
+        o = O_A[t]
+        k0 = 0 if t < 3 else 4
+        ts(sb("uout", o + 16 * k0, o + 80), ind(sb("tp"), sb("ol", OL_NEW + k0, OL_NEW + 5)), OFF - 1, A.add, XW - 1.0, A.min)
+        lst, lt = sb("uout", o, o + 64), sb("uout", o + 64, o + 68)
+        if t < 3: send([(lst, 1, sb("uin", U_A[(t + 1, t)], U_A[(t + 1, t)] + 64), "a%d" % t)])
+        tt(ind(mwin, ids), raw, go, A.subtract)
+        ts(sb("uout", O_M[t], O_M[t] + n), sb("mw", b, b + n), OFF, A.add)
+        ts(sb("uout", O_M[t] + n, O_M[t] + N), go, OFF, A.add)
+        send([(sb("uout", O_M[t], O_M[t] + N), 1, sb("uin", U_M[t + 1], U_M[t + 1] + N), "b%d" % t)])
+        tt(sb("xx", 64, 68), sb("tp", 128 + 15, 192, 16), sb("tp", 192 + 15, 256, 16), A.subtract)
+        tt(sb("xx", 0, 64), ind(sb("xx", 64, 68), sb("ol", OL_X, OL_X + 4)), sb("pm"), A.mult)
+        mms(total([(v3(pm, 128, 192), sb("ea"), sb("xx", 0, 64))]) + total([(v3(pm, 192, 256), E("bf", 1), sb("xx", 0, 64))]))
+        act(sb("hv", 0, 64), v3(pm, 128, 192), F.Copy)
+        tt(sb("hv", 64, 128), sb("hv", 0, 64), v3(pm, 192, 256), A.add)
+        cp(ind(sb("ft"), lt), sb("hv", 64, 128))
+        old = n - 64 if t else n
+        act(sb("sg", b, b + old), sb(pe, 0, old), F.Sign, bias=1.0 - 2 * TA[t] - (KS if t else 0.0))
+        if t: act(sb("sg", b + old, b + n), sb("pd2", 0, 64), F.Sign, bias=17.0 - 2 * TA[t])
+        send([(sb("sg", b, b + n), 1, sb("sp", 512 * (t + 1), 512 * (t + 1) + n), "c%d" % t)])
+        live = sb("hv", 128, 192)
+        act(live, ind(swin, ids), F.Identity, bias=-2.0 * V, scale=-2.0 * V)
+        tt(gs(1), ind(ewin, ids), live, A.max)
+        ts(sb("fo"), gs(1), float(V), A.add)
+        more([(sb("px", 0, 64), idf, go), (sb("px", 0, 64), nidf, raw)], ("s", t), True)
+        more([(sb("px", 0, 64), idb, live)], ("s", t))
+        act(gs(2), sb("px", 0, 64), F.Relu, bias=V - OFF)
         fv = FG_V[t]
         if fv: cp(sb("fg", 0, 16 * fv), ind(sb("ft"), sb("fo", 0, fv)))
         if fv < 64: act(sb("fg", 16 * fv, 1024), ind(sb("ft"), sb("fo", fv, 64)), F.Copy)
-        if t < 3:
-            mm(v3("pd3", 0, 64), sb("idf"), gs(6), ("nt", t), True)
-            for c in range(16):
-                mm(v3("pd3", 0, 64), E("b1", c), sb("fg", c, 1024, 16), ("nt", t))
-            ts(sb("uout", o + 80, o + 144), v3("pd3", 0, 64), -1.0, A.mult, float(V), A.add)
-        pn = "pd2"
-        mm(v3(pn, 256, 320), sb("idf"), gs(3), ("nn", t), True)
-        mm(v3(pn, 256, 320), sb("idf"), gs(5), ("nn", t))
-        for i in range(16):
-            mm(v3(pn, 256, 320), E("b1", i), sb("fg", 64 * i, 64 * i + 64) if t < 3 else sb("fg", i, 1024, 16), ("nn", t))
-        if t < 3:
-            cp(sb("uout", o + 144, o + 208), v3(pn, 256, 320))
-            u = U_NEW[(t + 1, t)]
-            send(sb("uout", o + 80, o + 208), [(1, sb("uin", u + 80, u + 208), "d%d" % t)], 32)
-            far = [(k - t, sb("uin", U_NEW[(k, t)] + 4, U_NEW[(k, t)] + 144), "f%d%d" % (t, k)) for k in range(t + 2, 4)]
-            send(sb("uout", o + 4, o + 144), far, 35)
-            cp(ind(sb("ft"), lt), sb("zero", 0, 64))
-        else:
-            ts(sb("lasto"), v3(pn, 256, 320), -1.0, A.mult, float(V), A.add)
-            send(sb("lasto"), [(1, sb("lasti"), "d3")], 32)
+        more([(sb("px", 64, 128), idf, gs(1)), (sb("px", 64, 128), nidf, gs(2))], ("n", t), True)
+        more([(sb("px", 64, 128), E("b1", i), sb("fg", i, 1024, 16)) for i in range(16)], ("n", t))
+        new = sb("uin", U_H, U_H + 64) if t == 0 else sb("uout", O_D[t], O_D[t] + 64)
+        ts(new, sb("px", 64, 128), float(V), A.add)
+        home = sb("uin", U_H + 64 * t, U_H + 64 * t + 64)
+        if t == 3:
+            send([(new, 1, home, "d3")])
+            return
+        land = lambda k: sb("uin", U_TS[k] + TSW + 64 * t, U_TS[k] + TSW + 64 * t + 64)
+        send([(new, 1, land(t + 1), "d%d" % t)])
+        far = []
+        for k in range(t + 2, 4):
+            far += [(lst, k - t, sb("uin", U_A[(k, t)], U_A[(k, t)] + 64), "a%d%d" % (t, k)), (new, k - t, land(k), "d%d%d" % (t, k))]
+        if t: far.append((new, 4 - t, home, "h%d" % t))
+        send(far)
+        for k in range(2):
+            dma("Y", (T.ft[k:128:16, :], ("ft", k, k + 1), XW), T.ft[k + 2:128:16, :], 64)
 
     early(0)
     for t in range(NT):
         if t + 1 < NT: early(t + 1)
         decide(t)
-    ts(sb("mf"), sb("uin", U_M[4], U_M[4] + 512), -1.0, A.mult, float(V), A.add)
+    ts(sb("mf"), sb("uin", U_M[4], U_M[4] + 512), float(V), A.min)
     dma("Y", T.ym[:], sb("mf"), 256)
-    ts(sb("ef"), sb("uin", U_E[4], U_E[4] + 448), -1.0, A.mult, float(V), A.add)
-    dma("Y", T.yi[:, 0:448], sb("ef"), 224)
-    dma("Y", T.yi[:, 448:512], sb("lasti"), 32)
+    cp(sb("eh", 256, 448), sb("uin", U_H, U_H + 192))
+    more([(sb("pe0", 0, 448), i2k, sb("neg"))], ("f",), True)
+    more([(sb("pe0", 0, 448), i2k, sb("sp", 2048, 2048 + 448))], ("f",))
+    tt(sb("ef", 0, 448), sb("eh"), sb("pe0", 0, 448), A.max)
+    dma("Y", T.yi[:, 0:448], sb("ef", 0, 448), 224)
+    cp(sb("ef", 448, 512), sb("uin", U_H + 192, U_H + 256))
+    dma("Y", T.yi[:, 448:512], sb("ef", 448, 512), 32)
     return ops
 
 
@@ -492,25 +568,108 @@ def one_pass(ops, pred, succ, prio, back):
     return st, fin
 
 
-def schedule(ops):
+def span(ops, order, other, wait):
+    free, fin = {}, [0.0] * len(ops)
+    for i in order:
+        o = ops[i]
+        t = free.get(o["q"], 0.0)
+        for d, k in o["deps"].items():
+            u = fin[d] + (wait if k == "wait" else 0.0)
+            if u > t: t = u
+        t += other[i]["cost"]
+        if o["q"] != "R": free[o["q"]] = t
+        fin[i] = t + other[i]["lat"]
+    return max(fin)
+
+
+def schedule(ops, others):
     n = len(ops)
-    pred = [[(d, T_SEM if k == "wait" else 0.0) for d, k in o["deps"].items()] for o in ops]
+    pred = [[(d, COSTS[0][-1] if k == "wait" else 0.0) for d, k in o["deps"].items()] for o in ops]
     succ = [[] for _ in ops]
     for i in range(n):
         for d, gap in pred[i]: succ[d].append((i, gap))
     prio = [0.0] * n
     for i in reversed(range(n)):
         prio[i] = ops[i]["cost"] + ops[i]["lat"] + max([prio[s] + gap for s, gap in succ[i]] + [0.0])
-    z, best = SEED, None
-    for _ in range(PASSES):
-        for i in range(n):
-            z = (z * 1103515245 + 12345) % 2147483648
-            prio[i] += JIT * z / 2147483648.0
-        st, fin = one_pass(ops, pred, succ, prio, False)
-        if best is None or max(fin) < best[0]: best = (max(fin), st)
-        prio = one_pass(ops, succ, pred, fin, True)[1]
-    for i in range(n): ops[i]["st"] = best[1][i]
-    return sorted(ops, key=lambda o: (o["st"], o["id"]))
+    z, best, base = SEED, None, None
+    for it in range(TRIES):
+        if it % 7 == 6:
+            p = one_pass(ops, succ, pred, best[2], True)[1]
+        else:
+            p = prio[:]
+            for _ in range((n // 7, 8, 1)[it % 3] if it else 0):
+                z = (z * 1103515245 + 12345) % 2147483648
+                a = z // 4096 % n
+                for i in range(a, min(n, a + (1, 1, (3, 8, 20, 50)[it % 4])[it % 3])):
+                    p[i] += (z % 4096 - 2048) / (1600.0, 600.0, 600.0)[it % 3]
+        st, fin = one_pass(ops, pred, succ, p, False)
+        order = sorted(range(n), key=lambda i: (st[i], i))
+        times = [span(ops, order, o, c[-1]) for o, c in zip(others, COSTS)]
+        base = base or times
+        score = sum(a / b for a, b in zip(times, base)) + times[0] / base[0]
+        if best is None or score < best[0]: best, prio = (score, order, fin, st, times), p
+    order = polish(ops, others, best[1])
+    return order, [span(ops, order, o, c[-1]) for o, c in zip(others, COSTS)]
+
+
+def polish(ops, others, order):
+    n, names = len(ops), "VSPGYR"
+    q = [names.index(o["q"]) for o in ops]
+    dep = [[(d, k == "wait") for d, k in o["deps"].items()] for o in ops]
+    dset = [set(o["deps"]) for o in ops]
+    sets = [([x["cost"] for x in others[m]], [x["lat"] for x in others[m]], COSTS[m][-1]) for m in POLISH]
+
+    def run(order, c, lat, w, pairs=None):
+        free, last, fin, why = [0.0] * 6, [-1] * 6, [0.0] * n, [None] * n
+        for i in order:
+            k = q[i]
+            t, y, v = free[k], last[k], True
+            for d, s in dep[i]:
+                u = fin[d] + w if s else fin[d]
+                if u > t: t, y, v = u, d, False
+            t += c[i]
+            if k != 5: free[k], last[k] = t, i
+            fin[i], why[i] = t + lat[i], (y, v)
+        end = max(fin)
+        i = fin.index(end)
+        while pairs is not None and i >= 0:
+            if why[i][1] and why[i][0] >= 0: pairs.append((why[i][0], i))
+            i = why[i][0]
+        return end
+
+    z = [SEED]
+
+    def draw(k):
+        z[0] = (z[0] * 1103515245 + 12345) % 2147483648
+        return z[0] // 16 % k
+
+    base = [run(order, *s) for s in sets]
+    cur, best, pairs = 1.0, (1.0, order), None
+    for it in range(STEPS):
+        if pairs is None:
+            pairs = []
+            run(order, *sets[draw(len(sets))], pairs)
+        a, b = pairs[draw(len(pairs))]
+        pa, pb = order.index(a), order.index(b)
+        if draw(2):
+            seg, move = order[pa:pb + 1], {b}
+            for x in reversed(seg):
+                if x in move: move |= dset[x]
+            if a in move: continue
+            new = order[:pa] + [x for x in seg if x in move] + [x for x in seg if x not in move] + order[pb + 1:]
+        else:
+            pe = min(n - 1, pb + (0, 0, 10, 30)[draw(4)])
+            seg, move = order[pa:pe + 1], {a}
+            for x in seg:
+                if dset[x] & move: move.add(x)
+            if b in move: continue
+            new = order[:pa] + [x for x in seg if x not in move] + [x for x in seg if x in move] + order[pe + 1:]
+        score = sum(run(new, *s) / b0 for s, b0 in zip(sets, base)) / len(sets)
+        if score < cur - HEAT * (1.0 - it / STEPS) * math.log((draw(9999) + 1) / 10000.0):
+            order, cur, pairs = new, score, None
+            if score < best[0]: best = (score, new)
+        elif draw(10) == 0: pairs = None
+    return best[1]
 
 
 def emit(g, T, ops, order):
@@ -548,8 +707,9 @@ def emit(g, T, ops, order):
                 qs[q].wait_ge(T.sem[s], v)
                 for s2, v2 in clock[d].items(): kn[s2] = max(kn.get(s2, 0), v2)
         if q == "P":
-            out, l, r, first = o["mm"]
-            ins = g.tensor.matmul(out, l, r, first, lastg[o["grp"]] == o["id"])
+            for k, (out, l, r, start, stop) in enumerate(o["mm"]):
+                if o["shared"]: stop = lastg[o["grp"]] == o["id"] and k == len(o["mm"]) - 1
+                ins = g.tensor.matmul(out, l, r, start, stop)
         else:
             ins = o["fn"](g)
         ck = dict(kn)
@@ -565,10 +725,15 @@ def emit(g, T, ops, order):
         g.wait_ge(T.sem[s], v)
 
 
+ORDER = []
+
+
 def rank_program(g, core, T, topo):
     rank = T.rank_of(core)
     if rank is None:
         return
     ops = build(T, topo, core, rank)
     link(ops)
-    emit(g, T, ops, schedule(ops))
+    if not ORDER:
+        ORDER.extend(schedule(ops, [build(T, topo, core, rank, c) for c in COSTS])[0])
+    emit(g, T, ops, [ops[i] for i in ORDER])

import math

from concourse.bass import DstId, RemoteDMATransfer
from concourse.mybir import AluOpType as A, ActivationFunctionType as F

V, S0, C, NT = 4096, 256, 64, 4
TA, TB = (12, 13, 12, 14), (10, 11, 9, 11)
VS = 96
SS = S0 - VS
ON_V = [True, True, True, True]
S_PARTS = [(160, 40, (3, 3, 3, 3, 2, 2))]
V_PART = (VS, VS // 2, (5, 5, 3, 3))
OLD_GATHER = 32
V_GATHERS = []
V_SIGNS = []
M_RUNS = [(1,) * 5 + (2,) * 5, (1,) + (2,) * 7, (1,) + (2,) * 7, (1,) + (2,) * 7]
OLD_RUNS = (8, 6)
FG_V = [0, 0, 0, 32]
XW = 4176
OFF = 65535.0
KS = 64.0

TSW = 256 + VS + 256
U_TS, U_A, _c = {}, {}, 0
for _t in range(4):
    U_TS[_t] = _c
    _c += TSW + C * _t
for _t in range(1, 4):
    for _j in range(_t):
        U_A[(_t, _j)] = _c
        _c += 64
U_M = [_c + 512 * t for t in range(5)]
_c += 512 * 5
U_H = _c
UW = _c + 256
O_A = [80 * t for t in range(4)]
O_D = [320 + 64 * t for t in range(4)]
O_M = [576 + 512 * t for t in range(4)]
OW = 576 + 2048
CW = 15 * 256 + 14 * 192 + 16 * 448
XE = 16 * 448
XL = 768 + 3 * VS + 3 * 512
OL_NEW, OL_VS, OL_X = 18, 24, 24 + VS // 16 + VS // 16 % 2
OLW = OL_X + 4

SCRATCH = {
    "xw": ("sbuf", [128, XW], "bfloat16"), "ft": ("sbuf", [128, XW], "bfloat16"),
    "mi": ("sbuf", [128, 256], "int32"), "ei": ("sbuf", [128, 256], "int32"),
    "uin": ("sbuf", [128, UW], "uint16"), "uout": ("sbuf", [128, OW], "uint16"),
    "cmp": ("sbuf", [128, 2 * CW], "bfloat16"), "xe": ("sbuf", [128, 2 * XE], "bfloat16"),
    "xl": ("sbuf", [128, 4 * XL], "bfloat16"),
    "mw": ("sbuf", [128, 2048], "float32"), "ew": ("sbuf", [128, 2048], "float32"),
    "ww": ("sbuf", [128, 2048], "bfloat16"), "sg": ("sbuf", [128, 2048], "bfloat16"), "sp": ("sbuf", [128, 2560], "bfloat16"),
    "hw": ("sbuf", [128, 40], "bfloat16"), "cs": ("sbuf", [128, 160], "bfloat16"), "c2": ("sbuf", [128, 128], "bfloat16"),
    "fi": ("sbuf", [128, 64], "bfloat16"), "ids": ("sbuf", [128, 64], "uint16"),
    "g1": ("sbuf", [128, 2, 64], "float32"), "gs": ("sbuf", [128, 192], "float32"),
    "tp": ("sbuf", [128, 256], "float32"), "t0": ("sbuf", [128, 1024], "float32"),
    "xx": ("sbuf", [128, 128], "float32"), "hv": ("sbuf", [128, 192], "bfloat16"),
    "fo": ("sbuf", [128, 64], "uint16"), "fg": ("sbuf", [128, 1024], "bfloat16"),
    "mf": ("sbuf", [128, 512], "float32"), "ef": ("sbuf", [128, 512], "float32"), "eh": ("sbuf", [128, 448], "float32"),
    "pi": ("sbuf", [128, 1], "int32"), "ci": ("sbuf", [128, 8], "int32"), "cf": ("sbuf", [128, 16], "float32"),
    "jf": ("sbuf", [128, 160], "float32"), "jc": ("sbuf", [128, 64], "float32"),
    "row": ("sbuf", [128, 16 * (OLW + 2)], "bfloat16"), "ol": ("sbuf", [128, OLW + 2], "uint16"),
    "b1": ("sbuf", [128, 144], "bfloat16"), "b2": ("sbuf", [128, 144], "bfloat16"),
    "bf": ("sbuf", [128, 144], "float32"), "ea": ("sbuf", [128, 128], "float32"),
    "idb": ("sbuf", [128, 128], "bfloat16"), "dg": ("sbuf", [128, 9 * 128], "bfloat16"), "df": ("sbuf", [128, 3 * 128], "float32"),
    "bo": ("sbuf", [128, 4 * 128], "bfloat16"), "rr": ("sbuf", [128, 288], "float32"), "rb": ("sbuf", [128, 288], "bfloat16"),
    "ones": ("sbuf", [128, 448], "bfloat16"), "neg": ("sbuf", [128, 448], "bfloat16"), "fl": ("sbuf", [128, 256 + 3 * 136], "bfloat16"),
    "cst": ("sbuf", [128, 448], "bfloat16"), "thr": ("sbuf", [128, 128], "bfloat16"), "seg": ("sbuf", [128, 128], "bfloat16"),
    "rst": ("sbuf", [128, 160], "bfloat16"), "pm": ("sbuf", [128, 64], "float32"),
}
PS = ["pm0", "pm1", "pe0", "pe1", "pd0", "pd1", "pd2", "px"]
for _n in PS:
    SCRATCH[_n] = ("psum", [128, 16, 32] if _n[:2] == "pm" else [128, 512], "float32")
EPS = 2.0 ** -115

MSG = ["ts1", "ts2", "ts3"] + ["%s%d" % (k, t) for t in range(3) for k in "abcd"] + ["b3", "c3", "d3"]
MSG += ["a02", "a03", "d02", "d03", "a13", "d13", "h1", "h2"]
SEMAPHORES = ["qv", "qs", "qp", "qg", "sent"] + ["r_" + m for m in MSG] + ["l%d" % k for k in range(48)]
QSEM = {"V": "qv", "S": "qs", "P": "qp", "G": "qg"}

COSTS = [(0.00083, 0.00042, 0.003, 1.56, 3.5, 3.0, 0.5, 0.05, 0.1), (0.001, 0.00053, 0.0, 1.1, 2.5, 2.0, 0.4, 0.03, 0.05),
         (0.00083, 0.00057, 0.0, 1.5, 3.5, 2.5, 0.6, 0.02, 0.08), (0.0009, 0.00045, 0.003, 1.3, 3.5, 3.0, 0.5, 0.05, 0.12),
         (0.0011, 0.00055, 0.0, 1.9, 5.0, 2.0, 0.5, 0.05, 0.08), (0.001, 0.0005, 0.01, 1.5, 3.0, 4.0, 0.8, 0.05, 0.1)]
T_DMA, DBW = 2.0, 300.0
LOOK, SEED, TRIES = 0.25, 1, 200
POLISH, STEPS, HEAT = (0, 1, 4), 25000, 0.0007


def build(T, topo, core, rank, costs=None):
    CY, PCY, PF, GA, SCA, T_HOP, T_RISS, VF, _ = costs or COSTS[0]
    ops = []

    def sb(name, a=0, b=None, step=None):
        w = T[name].shape[1]
        b = w if b is None else b
        return (T[name][:, a:b] if step is None else T[name][:, a:b:step], (name, a, b), len(range(a, b, step or 1)))

    def v3(name, a, b, h=None):
        t = T[name][:, a // 32:b // 32, :] if h is None else T[name][:, a // 32:b // 32, 16 * h:16 * h + 16]
        return (t, (name, a, b), (b - a) // (1 if h is None else 2))

    def blk(name, k, a, b):
        return (T[name][:, k, a:b], (name, 32 * k + a, 32 * k + b), b - a)

    def ind(win, off):
        return (win[0].indirect(off[0]), [win[1], off[1]], 16 * off[2], "ind")

    def regs(xs):
        out = []
        for x in xs:
            if isinstance(x, tuple):
                out += x[1] if isinstance(x[1], list) else [x[1]]
        return out

    def val(x):
        return x[0] if isinstance(x, tuple) else x

    def two(*xs):
        return all(SCRATCH[r[0]][2] in ("bfloat16", "uint16") for r in regs(xs))

    def add(q, fn, outs, ins, cost, **kw):
        rd, wr = regs(ins), regs(outs)
        for o in outs:
            if len(o) == 4:
                wr.remove(o[1][1]); rd.append(o[1][1])
        d = dict(q=q, fn=fn, rd=rd, wr=wr, cost=cost, lat=0.0, id=len(ops), deps={}, grp=None, acc=False, tok=None)
        d.update(kw)
        ops.append(d)
        return d

    def vcost(out, first, k):
        if len(out) == 4: return 0.05 + out[2] * SCA * CY
        if len(first) == 4: return 0.05 + first[2] * GA * CY
        return VF + max(64, first[2] * k) * CY

    def cp(out, a):
        return add("V", lambda g: g.vector.tensor_copy(out[0], a[0]), [out], [a], vcost(out, a, 0.5 if two(out, a) else 1))

    def ts(out, a, s1, o1, s2=None, o2=None):
        if o2 is None: fn = lambda g: g.vector.tensor_scalar(out[0], a[0], val(s1), None, o1)
        else: fn = lambda g: g.vector.tensor_scalar(out[0], a[0], val(s1), val(s2), o1, o2)
        return add("V", fn, [out], [a, s1, s2], vcost(out, a, 0.5 if two(out, a) else 1))

    def tt(out, a, b, o):
        k = 1 if any(r[0] in PS for r in regs([a, b])) else 2
        return add("V", lambda g: g.vector.tensor_tensor(out[0], a[0], b[0], o), [out], [a, b], vcost(out, a, k))

    def scan(out, a, b, o0, o1):
        return add("V", lambda g: g.vector.tensor_tensor_scan(out[0], a[0], b[0], 0.0, o0, o1), [out], [a, b],
                   vcost(out, a, 0.5 if two(out, a, b) else 1))

    def tr(out, a):
        return add("V", lambda g: g.vector.transpose(out[0], a[0]), [out], [a], vcost(out, a, 1))

    def act(out, a, f, bias=0.0, scale=1.0):
        fn = lambda g: g.scalar.activation(out[0], a[0], f, bias=val(bias), scale=val(scale))
        cost = 0.065 + a[2] * GA * CY if len(a) == 4 else VF + max(64, a[2]) * CY
        return add("S", fn, [out], [a, bias, scale], cost)

    def mms(items, grp=None):
        cost = sum(PF + max(min(64, l[2]), r[2]) * (4 if SCRATCH[l[1][0]][2] == "float32" else 1) * PCY for _, l, r, _, _ in items)
        d = add("P", None, [i[0] for i in items], [x for i in items for x in i[1:3]], cost, grp=grp or len(ops), acc=not items[0][3])
        d["mm"] = [(o[0], l[0], r[0], a, b) for o, l, r, a, b in items]
        d["shared"] = grp is not None
        return d

    def total(terms):
        return [t + (k == 0, k == len(terms) - 1) for k, t in enumerate(terms)]

    def apart(terms, grp, first=False):
        d = mms([t + (True, True) for t in terms], grp)
        d["shared"], d["acc"] = False, not first

    def more(terms, grp, first=False):
        return mms([t + (first and k == 0, False) for k, t in enumerate(terms)], grp)

    def iota(out, pat, base, cm=0):
        if SCRATCH[out[1][0]][2] == "int32": fn = lambda g: g.iota(out[0], pat, base, cm)
        else: fn = lambda g: g.iota(out[0], pat, base, cm, allow_small_or_imprecise_dtypes=True)
        return add("G", fn, [out], [], 0.13 + 2 * out[2] * CY)

    def fill(out, c):
        return iota(out, [[0, out[2]]], c)

    def select(out, a, op, pat, base, cm):
        fn = lambda g: g.affine_select(out[0], a[0], pat, op, 0.0, base, cm)
        return add("G", fn, [out], [a], 0.17 + 2 * a[2] * CY)

    nl = [0]

    def dma(q, out, a, kb):
        s = "l%d" % nl[0]; nl[0] += 1
        if q == "Y": fn = lambda g: g.sync.dma_start(val(out), val(a)).then_inc(T.sem[s], 16)
        else: fn = lambda g: g.scalar.dma_start(val(out), val(a)).then_inc(T.sem[s], 16)
        outs = [out] if isinstance(out, tuple) else []
        return add(q, fn, outs, [a], 0.06, lat=T_DMA + kb / DBW, tok=(s, 16))

    def share(a, b, k, n):
        parts = [topo.engines(a, b)]
        while len(parts) < n:
            i = max(range(len(parts)), key=lambda i: (len(parts[i]), i))
            e = parts.pop(i)
            parts[i:i] = [e[:len(e) // 2], e[len(e) // 2:]]
        return parts[k]

    def send(items):
        n, trs, cnt = len(items), [], 0
        for k, (src, ahead, land, m) in enumerate(items):
            c = T.cores[(rank + ahead) % len(T.cores)]
            rid, pid, _ = topo.addr(c)
            eng = share(core, c, k, n)
            cnt += len(eng)
            trs.append((land[0], src[0], T.sem["r_" + m], pid, rid, sum(1 << e for e in eng)))
        if n == 1:
            d, s, sem, pid, rid, mk = trs[0]
            fn = lambda g: g.remote_dma(d, s, sem, T.sem.sent, pid, rid, mk)
        else:
            fn = lambda g: g.remote_dma_fused([RemoteDMATransfer(dst_ids=[DstId(rid=rid, pnc=pid)], dma_engine_mask=mk, remote_sem=sem,
                                                                 src=s, dst=d) for d, s, sem, pid, rid, mk in trs], local_sem=T.sem.sent)
        call = add("G", fn, [], [i[0] for i in items], T_RISS, tok="none", sent=cnt)
        for k, (src, ahead, land, m) in enumerate(items):
            back = T.cores[(rank - ahead) % len(T.cores)]
            r = add("R", None, [land], [], 0.0, lat=T_HOP + n * src[2] / 320.0, tok=("r_" + m, len(share(back, core, k, n))))
            r["after"] = call["id"]

    col = lambda k: sb("cf", k, k + 1)
    E = lambda name, i: sb(name, 15 - i, 143 - i)
    D = lambda k: sb("dg", 128 * k, 128 * k + 128)
    gi = sb("bo", 0, 128, 16)
    idb, idn, i16, i64, i2k, i65 = sb("idb"), D(0), D(1), D(2), D(3), D(4)
    idf, nidf = [sb("df", 128 * k, 128 * k + 128) for k in range(2)]
    bo, nbo, lo, up = [sb("bo", 128 * k, 128 * k + 128) for k in range(4)]

    dma("Y", sb("mi"), T.mem0[:], 128)
    dma("S", sb("ei"), T.inv0[:], 128)
    dma("Y", sb("xw", 0, 2048), T.xs[:, 0:2048], 700)
    dma("S", sb("xw", 2048, 4096), T.xs[:, 2048:4096], 1000)
    iota(sb("pi"), [[0, 1]], 0, 1)
    iota(sb("jf"), [[1, 160]], 0)
    for k, m in enumerate((15, 112, 96, 16)):
        ts(sb("ci", k, k + 1), sb("pi"), m, A.bitwise_and)
    cp(sb("cf", 0, 4), sb("ci", 0, 4))
    ts(col(6), col(2), col(0), A.subtract, 31.0, A.add)
    ts(col(7), col(3), 0.0, A.is_equal)
    ts(col(8), col(3), 0.0, A.is_gt)
    for e in range(2):
        ts(sb("rr", 144 * e, 144 * e + 144), sb("jf", 0, 144), col(6), A.is_equal, col(7 + e), A.mult)
    act(sb("rb"), sb("rr"), F.Copy)
    ts(sb("b1"), sb("jf", 0, 144), col(1), A.subtract, 15.0, A.is_equal)
    act(sb("b2"), sb("b1"), F.Copy, scale=2.0)
    act(sb("bf"), sb("b1"), F.Copy)
    fill(sb("ea"), 0)
    for k in range(2):
        act(sb("ea", k, 128, 16), sb("b1", 15, 143, 16), F.Copy, scale=1.0 - 2 * k)
    fill(sb("ones", 0, 160), 1)
    fill(sb("ones", 160, 448), 1)
    select(idb, sb("ones", 0, 128), A.is_equal, [[-1, 128]], 0, 1)
    for k, s in enumerate((-1.0, 16.0, KS, -V / 2.0, -16.0 * V)):
        act(D(k), idb, F.Copy, scale=s)
    for k, s in enumerate((1.0, -1.0)):
        act(sb("df", 128 * k, 128 * k + 128), idb, F.Copy, scale=s)
    r0 = 16 * OL_NEW
    iota(sb("row", 0, 256), [[-1, 16], [16, 2], [32, 8]], 14)
    iota(sb("row", 256, 288), [[0, 2], [16, 2], [32, 8]], 15)
    iota(sb("row", r0, r0 + 8), [[0, 2], [16, 2], [32, 2]], 128 + 15)
    iota(sb("row", r0 + 8, r0 + 64), [[-1, 14], [16, 2], [32, 2]], 13)
    iota(sb("row", r0 + 64, r0 + 96), [[0, 8], [16, 2], [32, 2]], 192 + 15)
    iota(sb("row", 16 * OL_VS, 16 * OL_VS + VS), [[-1, 16], [16, 2], [32, VS // 32]], 15)
    if 16 * OL_X > 16 * OL_VS + VS: fill(sb("row", 16 * OL_VS + VS, 16 * OL_X), 0)
    iota(sb("row", 16 * OL_X, 16 * OL_X + 64), [[1, 2], [2, 2], [0, 16]], 0)
    for a, b, ps in ((0, OL_NEW, "px"), (OL_NEW, OLW, "pd2")):
        mms(total([(sb(ps, a, b), E("b1", c), sb("row", 16 * a + c, 16 * b, 16)) for c in range(16)]))
        ts(sb("ol", a, b), sb(ps, a, b), 1.0 / 16, A.mult)
    act(sb("xw", V, XW), sb("ones", 0, XW - V), F.Copy, scale=-2.0 ** 99)
    act(sb("xw", V, XW), sb("xw", V, XW), F.Copy, scale=4.0)
    iota(sb("jc"), [[0, 4], [1, 16]], 0)
    select(lo, sb("ones", 0, 128), A.is_ge, [[-16, 8], [0, 16]], 0, 1)
    select(bo, lo, A.is_ge, [[16, 8], [0, 16]], 15, -1)
    act(nbo, bo, F.Copy, scale=-KS)
    select(lo, bo, A.is_ge, [[1, 128]], 0, -1)
    select(up, bo, A.is_gt, [[-1, 128]], 0, 1)
    act(sb("jc"), sb("jc"), F.Abs, bias=col(0), scale=-1.0)
    act(sb("pm"), sb("jc"), F.Relu, bias=1.0, scale=-1.0)
    fill(sb("fl", 256, 256 + 3 * 136), 0)
    fill(sb("cst", 0, SS), 16)
    fill(sb("cst", SS, S0), 0)
    fill(sb("cst", S0, 448), 16)
    fill(sb("neg"), -1)
    fill(sb("thr"), 0)
    act(col(11), col(0), F.Identity, bias=KS / 2, scale=KS)
    act(sb("thr", 0, 128, 32), sb("jf", 0, 4), F.Identity, bias=col(11), scale=16 * KS)
    iota(sb("seg"), [[0, 4], [1, 32]], 0)
    select(sb("rst"), sb("ones", 0, 160), A.is_gt, [[0, 5], [1, 32]], 0, 0)
    fill(sb("hw", 0, 8), 0)
    fill(sb("hw", 8, 40), 1)
    for t in range(NT):
        n = 512 * t + S0 + C * t
        iota(sb("mw", n, n + 64), [[1, 64]], V + 1 - int(OFF))
        for nm, c in (("ew", 0), ("ww", 0), ("sg", -1)):
            fill(sb(nm, n, n + 64), c)
    for k in range(8):
        fill(sb("ft", k * (XW // 8), (k + 1) * (XW // 8)), 0)

    def arrange(ps, c0, w, half, one, plus=None):
        side = [[(v3(ps, c0, c0 + w, e), sb(rr, 144 * e + 16 - 16 * h, 144 * e + 144 - 16 * h), f(h))
                 for rr, f in (("rr", half), ("rb", plus)) if f for h in range(2)] for e in range(2)]
        if one: mms(total([(v3(ps, c0, c0 + w), idb, sb("ones", 0, w))] + side[0] + side[1]))
        else: mms(total(side[0]) + total(side[1]))

    u0 = U_TS[0]
    ts(sb("t0", 0, 256), sb("mi"), V - 1.0, A.min, OFF, A.subtract)
    ts(sb("fl", 0, 256), sb("mi"), float(V), A.is_equal, OFF - V + 1, A.mult)
    tt(sb("mw", 0, 256), sb("t0", 0, 256), sb("fl", 0, 256), A.add)
    arrange("pm1", 0, 256, lambda h: sb("t0", 128 * h, 128 * h + 128), True, lambda h: sb("fl", 128 * h, 128 * h + 128))
    tr(sb("t0", 256, 512), v3("pm1", 0, 256))
    scan(sb("t0", 512, 768), sb("t0", 256, 512), sb("t0", 256, 512), A.mult, A.min)
    ts(sb("uin", u0, u0 + 16), ind(sb("t0", 512, 768), sb("ol", 16, 17)), OFF - 1, A.add, XW - 1.0, A.min)
    ts(sb("uin", u0 + 16, u0 + 272), ind(sb("t0", 256, 512), sb("ol", 0, 16)), OFF - 1, A.add, XW - 1.0, A.min)
    ts(sb("ew", 0, 256), sb("ei"), float(V), A.subtract)
    cp(sb("uin", u0 + 256 + VS, u0 + TSW), sb("ei"))
    cp(sb("eh", 0, 256), sb("ei"))
    arrange("pm1", 256, VS, lambda h: sb("ew", SS + VS // 2 * h, SS + VS // 2 * (h + 1)), False)
    tr(sb("t0", 768, 768 + VS), v3("pm1", 256, 256 + VS))
    ts(sb("uin", u0 + 256, u0 + 256 + VS), ind(sb("t0", 768, 768 + VS), sb("ol", OL_VS, OL_VS + VS // 16)), float(V), A.add)
    for k in (1, 2, 3):
        send([(sb("uin", u0, u0 + TSW), k, sb("uin", U_TS[k], U_TS[k] + TSW), "ts%d" % k)])

    xwin = sb("xw", 0, XW)
    bank = [0]

    def members(t, j):
        pm, x0, cb = "pm%d" % (t % 2), XL * t, CW * (t % 2)
        if j is None:
            u, w, c0, first = U_TS[t], 256, 0, 1
            xe = x0 + 768
            act(sb("xl", xe - 256, xe), ind(xwin, sb("uin", u, u + 16)), F.Copy)
            for k in range(1, max(M_RUNS[t])):
                dma("Y", sb("xl", xe - 256 * (k + 1), xe - 256 * k), sb("xl", xe - 256, xe), 64)
            for k in range(3 if ON_V[t] else 0):
                dma("Y", sb("xl", xe + VS * k, xe + VS * (k + 1)), sb("xl", xe - VS, xe), 24)
            runs = M_RUNS[t]
        else:
            u, w, c0, first = U_A[(t, j)], 64, S0 + C * j, 2
            xe = x0 + 768 + 3 * VS + 512 * (j + 1)
            cb += 15 * 256 + 14 * 64 * j
            act(sb("xl", xe - 128, xe), ind(xwin, sb("uin", u, u + 8)), F.Copy)
            runs = (2,) * 7 if j == t - 1 else OLD_RUNS
            for k in range(1, max(runs) // 2):
                dma("Y", sb("xl", xe - 128 * (k + 1), xe - 128 * k), sb("xl", xe - 128, xe), 32)
        if j is None: cell = lambda i, h: (T[pm][:, 4 * h:4 * h + 4, i:32:16], (pm, 0, 256), 8)
        elif j < t - 1: cell = lambda i, h: (T[pm][:, c0 // 32:c0 // 32 + 2, i // 2:32:8], (pm, c0, c0 + 64), 8)
        else: cell = lambda i, h: sb("px", i // 2, 64, 8)
        grp = ("m", t, j == t - 1)
        apart([(cell(0, h), sb("ones", 0, 128), gi) for h in range(2 if j is None else 1)], grp, j is None or j == t - 1)
        k, i = w // 16, first
        for nr in runs:
            o, ln = cb + (i - first) * w, nr * w
            tt(sb("cmp", o, o + ln), ind(xwin, sb("uin", u + k * i, u + k * (i + nr))), sb("xl", xe - ln, xe), A.is_equal)
            apart([(cell(i + 128 * q // w, q % 2), sb("cmp", o + 128 * q, o + 128 * (q + 1)), gi) for q in range(ln // 128)], grp)
            i += nr

    def enough(t, js):
        pm, back = "pm%d" % (t % 2), []
        for j in js:
            if j is None:
                act(sb("fl", 0, 256), v3(pm, 0, 256), F.Relu, bias=1.0 - TB[t])
                for h in range(2):
                    back += total([(v3(pm, 128 * h, 128 * h + 128), sb("fl", 128 * h, 128 * h + 128), i65)])
            else:
                f, c0 = 256 + 136 * (j if j < t - 1 else 2), S0 + C * j
                act(sb("fl", f + 1, f + 129, 2), v3(pm, c0, c0 + 64) if j < t - 1 else sb("px", 0, 64), F.Relu, bias=1.0 - TB[t])
                back += total([(v3(pm, c0, c0 + 64), sb("fl", f + 1 - h, f + 129 - h), sb("dg", 512 + 64 * h, 576 + 64 * h)) for h in range(2)])
        mms(back)

    def bounds(t, j):
        par = t % 2
        pe, cb = "pe%d" % par, CW * par + 15 * 256 + 14 * 192
        if j is None:
            u, xv = U_TS[t] + 256, XL * t + 768 - VS
            for i in range(0, 16 if ON_V[t] else 0, 4):
                o = cb + 16 * SS + i * VS
                tt(sb("cmp", o, o + 4 * VS), ind(xwin, sb("uin", u + VS // 16 * i, u + VS // 16 * (i + 4))), sb("xl", xv, xv + 4 * VS), A.is_ge)
                more([(sb(pe, SS, S0), E("b2", i + r), sb("cmp", o + r * VS, o + (r + 1) * VS)) for r in range(4)], ("e", t, False))
            parts, c0 = [], 0
            for w, step, rows in S_PARTS + ([] if ON_V[t] else [V_PART]):
                parts.append((c0, w, XL * t + 512 + c0, 1, step, rows))
                c0 += w
        else:
            parts = [(S0 + C * j, 64, XL * t + 768 + 3 * VS + 512 * (j + 1) - 128, 2, 32 if j == t - 1 else OLD_GATHER, (8, 8))]
        for c0, w, x0, rep, step, rows in parts:
            u, xo, o = U_TS[t] + 256 + VS + c0, XE * par + 16 * c0, cb + 16 * c0
            for s in range(0, w, step):
                out, got = sb("xe", xo + 16 * s, xo + 16 * (s + step)), ind(xwin, sb("uin", u + s, u + s + step))
                if (t, j, s // step) in V_GATHERS: cp(out, got)
                else: act(out, got, F.Copy)
            i = 0
            for k, nr in enumerate(rows):
                if j is not None and j == t - 1: pd = ("pd2", "px")[k]
                else:
                    pd = "pd%d" % (bank[0] % 2); bank[0] += 1
                run = []
                for r in range(0, nr, rep):
                    run += total([(sb(pd, r * w, (r + rep) * w), idn, sb("xl", x0, x0 + rep * w))] +
                                 [(sb(pd, q * w, (q + 1) * w), idb, sb("xe", xo + i + q, xo + 16 * w, 16)) for q in range(r, r + rep)])
                mms(run)
                if (t, j, k) in V_SIGNS: ts(sb("cmp", o + i * w, o + (i + nr) * w), sb(pd, 0, nr * w), 0.0, A.is_ge, 0.5, A.subtract)
                else: act(sb("cmp", o + i * w, o + (i + nr) * w), sb(pd, 0, nr * w), F.Sign, bias=EPS)
                e = "b2" if (t, j, k) in V_SIGNS else "b1"
                new = j == t - 1
                more([(sb("pd2", 0, w) if new else sb(pe, c0, c0 + w), E(e, r), sb("cmp", o + r * w, o + (r + 1) * w))
                      for r in range(i, i + nr)], ("e", t, new), new and k == 0)
                i += nr

    def early(t):
        n, par = S0 + C * max(0, t - 1), t % 2
        more([(sb("pe%d" % par, 0, n), idb, sb("cst", 0, n)) if ON_V[t] else (sb("pe%d" % par, 0, n), i16, sb("ones", 0, n))],
             ("e", t, False), True)
        for j in [None] + list(range(t - 1)):
            members(t, j)
            bounds(t, j)
        enough(t, [None] + list(range(t - 1)))

    def decide(t):
        n, par, b = S0 + C * t, t % 2, 512 * t
        N = n + 64
        pm, pe = "pm%d" % par, "pe%d" % par
        gs = lambda k: sb("gs", 64 * k, 64 * k + 64)
        ue = U_TS[t] + 256 + VS
        if t:
            ts(sb("mw", b, b + n), sb("uin", U_M[t], U_M[t] + n), OFF, A.subtract)
            members(t, t - 1)
            enough(t, [t - 1])
            ts(sb("ew", b, b + n), sb("uin", ue, ue + n), float(V), A.subtract)
            more([(sb(pe, 0, n - 64), i64, sb("sp", 512 * t, 512 * t + n - 64))], ("e", t, False))
        tt(sb("ww", b, b + n), v3(pm, 0, n), sb("mw", b, b + n), A.is_gt)
        mms(total([(blk(pm, 0, 0, n // 16), E("b1", c), sb("ww", b + c, b + n, 16)) for c in range(16)]))
        act(sb("hw", 8, 8 + n // 16), blk(pm, 0, 0, n // 16), F.Sign)
        mms(total([(sb("px", 0, 128), idb, sb("thr"))] + [(sb("px", 32 * d + 1, 32 * d + 32), nbo, sb("hw", 8, 39)) for d in range(4)]) +
            total([(sb("px", 128, 160), lo, sb("hw", 8, 40)), (sb("px", 128, 160), up, sb("hw", 7, 39))]))
        scan(sb("cs"), sb("rst"), sb("px", 0, 160), A.mult, A.add)
        if t: bounds(t, t - 1)
        scan(sb("c2"), sb("cs", 0, 128), sb("seg", 0, 128), A.max, A.min)
        run, ids = sb("ids", 16 * t, 16 * t + 4), sb("ids", 16 * t + 8, 16 * t + 12)
        cp(run, sb("c2", 31, 128, 32))
        tt(sb("fi"), ind(sb("cs", 128, 160), run), sb("jf", 0, 64), A.is_le)
        mms(total([(blk(pm, 0, 0, 4), i16, sb("c2", 31, 128, 32))] + [(blk(pm, 0, 0, 4), E("b1", c), sb("fi", c, 64, 16)) for c in range(16)]))
        cp(ids, blk(pm, 0, 0, 4))
        mwin, ewin, wwin, swin = sb("mw", b, b + N), sb("ew", b, b + N), sb("ww", b, b + N), sb("sg", b, b + N)
        go, raw = (T.g1[:, 0], ("g1", 0, 64), 64), (T.g1[:, 1], ("g1", 64, 128), 64)
        act(raw, ind(mwin, ids), F.Copy)
        tt(go, ind(wwin, ids), raw, A.mult)
        arrange(pm, 0, 128, lambda h: (T.g1[:, :, 32 * h:32 * h + 32], ("g1", 0, 128), 64), True)
        tr(sb("tp", 0, 128), v3(pm, 0, 128))
        scan(sb("tp", 128, 256), sb("tp", 0, 128), sb("tp", 0, 128), A.mult, A.min)
        o = O_A[t]
        k0 = 0 if t < 3 else 4
        ts(sb("uout", o + 16 * k0, o + 80), ind(sb("tp"), sb("ol", OL_NEW + k0, OL_NEW + 5)), OFF - 1, A.add, XW - 1.0, A.min)
        lst, lt = sb("uout", o, o + 64), sb("uout", o + 64, o + 68)
        if t < 3: send([(lst, 1, sb("uin", U_A[(t + 1, t)], U_A[(t + 1, t)] + 64), "a%d" % t)])
        tt(ind(mwin, ids), raw, go, A.subtract)
        ts(sb("uout", O_M[t], O_M[t] + n), sb("mw", b, b + n), OFF, A.add)
        ts(sb("uout", O_M[t] + n, O_M[t] + N), go, OFF, A.add)
        send([(sb("uout", O_M[t], O_M[t] + N), 1, sb("uin", U_M[t + 1], U_M[t + 1] + N), "b%d" % t)])
        tt(sb("xx", 64, 68), sb("tp", 128 + 15, 192, 16), sb("tp", 192 + 15, 256, 16), A.subtract)
        tt(sb("xx", 0, 64), ind(sb("xx", 64, 68), sb("ol", OL_X, OL_X + 4)), sb("pm"), A.mult)
        mms(total([(v3(pm, 128, 192), sb("ea"), sb("xx", 0, 64))]) + total([(v3(pm, 192, 256), E("bf", 1), sb("xx", 0, 64))]))
        act(sb("hv", 0, 64), v3(pm, 128, 192), F.Copy)
        tt(sb("hv", 64, 128), sb("hv", 0, 64), v3(pm, 192, 256), A.add)
        cp(ind(sb("ft"), lt), sb("hv", 64, 128))
        old = n - 64 if t else n
        act(sb("sg", b, b + old), sb(pe, 0, old), F.Sign, bias=1.0 - 2 * TA[t] - (KS if t else 0.0))
        if t: act(sb("sg", b + old, b + n), sb("pd2", 0, 64), F.Sign, bias=17.0 - 2 * TA[t])
        send([(sb("sg", b, b + n), 1, sb("sp", 512 * (t + 1), 512 * (t + 1) + n), "c%d" % t)])
        live = sb("hv", 128, 192)
        act(live, ind(swin, ids), F.Identity, bias=-2.0 * V, scale=-2.0 * V)
        tt(gs(1), ind(ewin, ids), live, A.max)
        ts(sb("fo"), gs(1), float(V), A.add)
        more([(sb("px", 0, 64), idf, go), (sb("px", 0, 64), nidf, raw)], ("s", t), True)
        more([(sb("px", 0, 64), idb, live)], ("s", t))
        act(gs(2), sb("px", 0, 64), F.Relu, bias=V - OFF)
        fv = FG_V[t]
        if fv: cp(sb("fg", 0, 16 * fv), ind(sb("ft"), sb("fo", 0, fv)))
        if fv < 64: act(sb("fg", 16 * fv, 1024), ind(sb("ft"), sb("fo", fv, 64)), F.Copy)
        more([(sb("px", 64, 128), idf, gs(1)), (sb("px", 64, 128), nidf, gs(2))], ("n", t), True)
        more([(sb("px", 64, 128), E("b1", i), sb("fg", i, 1024, 16)) for i in range(16)], ("n", t))
        new = sb("uin", U_H, U_H + 64) if t == 0 else sb("uout", O_D[t], O_D[t] + 64)
        ts(new, sb("px", 64, 128), float(V), A.add)
        home = sb("uin", U_H + 64 * t, U_H + 64 * t + 64)
        if t == 3:
            send([(new, 1, home, "d3")])
            return
        land = lambda k: sb("uin", U_TS[k] + TSW + 64 * t, U_TS[k] + TSW + 64 * t + 64)
        send([(new, 1, land(t + 1), "d%d" % t)])
        far = []
        for k in range(t + 2, 4):
            far += [(lst, k - t, sb("uin", U_A[(k, t)], U_A[(k, t)] + 64), "a%d%d" % (t, k)), (new, k - t, land(k), "d%d%d" % (t, k))]
        if t: far.append((new, 4 - t, home, "h%d" % t))
        send(far)
        for k in range(2):
            dma("Y", (T.ft[k:128:16, :], ("ft", k, k + 1), XW), T.ft[k + 2:128:16, :], 64)

    early(0)
    for t in range(NT):
        if t + 1 < NT: early(t + 1)
        decide(t)
    ts(sb("mf"), sb("uin", U_M[4], U_M[4] + 512), float(V), A.min)
    dma("Y", T.ym[:], sb("mf"), 256)
    cp(sb("eh", 256, 448), sb("uin", U_H, U_H + 192))
    more([(sb("pe0", 0, 448), i2k, sb("neg"))], ("f",), True)
    more([(sb("pe0", 0, 448), i2k, sb("sp", 2048, 2048 + 448))], ("f",))
    tt(sb("ef", 0, 448), sb("eh"), sb("pe0", 0, 448), A.max)
    dma("Y", T.yi[:, 0:448], sb("ef", 0, 448), 224)
    cp(sb("ef", 448, 512), sb("uin", U_H + 192, U_H + 256))
    dma("Y", T.yi[:, 448:512], sb("ef", 448, 512), 32)
    return ops


def link(ops):
    seen = {}
    for o in ops:
        acc = [(r, False) for r in o["rd"]] + [(r, True) for r in o["wr"]]
        for r, w in acc:
            ps = r[0] in PS
            a, b = (0, 1) if ps else r[1:]
            for (p, pa, pb, pw) in seen.get(r[0], []):
                if p is o or pb <= a or b <= pa or not (w or pw or ps): continue
                if p["q"] == "P" and o["q"] == "P":
                    if p["grp"] != o["grp"] or not p["acc"]: o["deps"][p["id"]] = "order"
                elif ps and p["q"] == o["q"] and not (w or pw): continue
                else: o["deps"][p["id"]] = "wait"
        for r, w in acc:
            a, b = (0, 1) if r[0] in PS else r[1:]
            lst = seen.setdefault(r[0], [])
            if w and not (o["q"] == "P" and o["acc"]):
                lst[:] = [x for x in lst if not (a <= x[1] and x[2] <= b)]
            lst.append((o, a, b, w))
        if "after" in o: o["deps"][o["after"]] = "hop"


def one_pass(ops, pred, succ, prio, back):
    n = len(ops)
    left = [len(p) for p in pred]
    ready, free = {}, {}
    rt, st, fin = [0.0] * n, [0.0] * n, [0.0] * n
    for i in range(n):
        if not left[i]:
            ready.setdefault(ops[i]["q"], []).append(i)
            if back: rt[i] = ops[i]["lat"]
    for _ in range(n):
        best = None
        for q, lst in ready.items():
            if not lst: continue
            t0 = max(free.get(q, 0.0), min(rt[i] for i in lst))
            i = max((k for k in lst if rt[k] <= t0), key=lambda k: prio[k])
            for k in lst:
                if rt[k] > t0 and prio[k] > prio[i] and rt[k] - t0 < LOOK * ops[i]["cost"]: i = k
            if best is None or t0 < best[0]: best = (t0, max(t0, rt[i]), q, i)
        _, s, q, i = best
        ready[q].remove(i)
        o = ops[i]
        if q != "R": free[q] = s + o["cost"]
        st[i], fin[i] = s, s + o["cost"] + (0.0 if back else o["lat"])
        for k, gap in succ[i]:
            rt[k] = max(rt[k], fin[i] + gap + (ops[k]["lat"] if back else 0.0))
            left[k] -= 1
            if not left[k]: ready.setdefault(ops[k]["q"], []).append(k)
    return st, fin


def span(ops, order, other, wait):
    free, fin = {}, [0.0] * len(ops)
    for i in order:
        o = ops[i]
        t = free.get(o["q"], 0.0)
        for d, k in o["deps"].items():
            u = fin[d] + (wait if k == "wait" else 0.0)
            if u > t: t = u
        t += other[i]["cost"]
        if o["q"] != "R": free[o["q"]] = t
        fin[i] = t + other[i]["lat"]
    return max(fin)


def schedule(ops, others):
    n = len(ops)
    pred = [[(d, COSTS[0][-1] if k == "wait" else 0.0) for d, k in o["deps"].items()] for o in ops]
    succ = [[] for _ in ops]
    for i in range(n):
        for d, gap in pred[i]: succ[d].append((i, gap))
    prio = [0.0] * n
    for i in reversed(range(n)):
        prio[i] = ops[i]["cost"] + ops[i]["lat"] + max([prio[s] + gap for s, gap in succ[i]] + [0.0])
    z, best, base = SEED, None, None
    for it in range(TRIES):
        if it % 7 == 6:
            p = one_pass(ops, succ, pred, best[2], True)[1]
        else:
            p = prio[:]
            for _ in range((n // 7, 8, 1)[it % 3] if it else 0):
                z = (z * 1103515245 + 12345) % 2147483648
                a = z // 4096 % n
                for i in range(a, min(n, a + (1, 1, (3, 8, 20, 50)[it % 4])[it % 3])):
                    p[i] += (z % 4096 - 2048) / (1600.0, 600.0, 600.0)[it % 3]
        st, fin = one_pass(ops, pred, succ, p, False)
        order = sorted(range(n), key=lambda i: (st[i], i))
        times = [span(ops, order, o, c[-1]) for o, c in zip(others, COSTS)]
        base = base or times
        score = sum(a / b for a, b in zip(times, base)) + times[0] / base[0]
        if best is None or score < best[0]: best, prio = (score, order, fin, st, times), p
    order = polish(ops, others, best[1])
    return order, [span(ops, order, o, c[-1]) for o, c in zip(others, COSTS)]


def polish(ops, others, order):
    n, names = len(ops), "VSPGYR"
    q = [names.index(o["q"]) for o in ops]
    dep = [[(d, k == "wait") for d, k in o["deps"].items()] for o in ops]
    dset = [set(o["deps"]) for o in ops]
    sets = [([x["cost"] for x in others[m]], [x["lat"] for x in others[m]], COSTS[m][-1]) for m in POLISH]

    def run(order, c, lat, w, pairs=None):
        free, last, fin, why = [0.0] * 6, [-1] * 6, [0.0] * n, [None] * n
        for i in order:
            k = q[i]
            t, y, v = free[k], last[k], True
            for d, s in dep[i]:
                u = fin[d] + w if s else fin[d]
                if u > t: t, y, v = u, d, False
            t += c[i]
            if k != 5: free[k], last[k] = t, i
            fin[i], why[i] = t + lat[i], (y, v)
        end = max(fin)
        i = fin.index(end)
        while pairs is not None and i >= 0:
            if why[i][1] and why[i][0] >= 0: pairs.append((why[i][0], i))
            i = why[i][0]
        return end

    z = [SEED]

    def draw(k):
        z[0] = (z[0] * 1103515245 + 12345) % 2147483648
        return z[0] // 16 % k

    base = [run(order, *s) for s in sets]
    cur, best, pairs = 1.0, (1.0, order), None
    for it in range(STEPS):
        if pairs is None:
            pairs = []
            run(order, *sets[draw(len(sets))], pairs)
        a, b = pairs[draw(len(pairs))]
        pa, pb = order.index(a), order.index(b)
        if draw(2):
            seg, move = order[pa:pb + 1], {b}
            for x in reversed(seg):
                if x in move: move |= dset[x]
            if a in move: continue
            new = order[:pa] + [x for x in seg if x in move] + [x for x in seg if x not in move] + order[pb + 1:]
        else:
            pe = min(n - 1, pb + (0, 0, 10, 30)[draw(4)])
            seg, move = order[pa:pe + 1], {a}
            for x in seg:
                if dset[x] & move: move.add(x)
            if b in move: continue
            new = order[:pa] + [x for x in seg if x not in move] + [x for x in seg if x in move] + order[pe + 1:]
        score = sum(run(new, *s) / b0 for s, b0 in zip(sets, base)) / len(sets)
        if score < cur - HEAT * (1.0 - it / STEPS) * math.log((draw(9999) + 1) / 10000.0):
            order, cur, pairs = new, score, None
            if score < best[0]: best = (score, new)
        elif draw(10) == 0: pairs = None
    return best[1]


def emit(g, T, ops, order):
    qs = {"V": g.vector, "S": g.scalar, "P": g.tensor, "G": g, "Y": g.sync}
    pos = {}
    for k, o in enumerate(order): pos[o["id"]] = k
    need, lastg = set(), {}
    for o in order:
        top = {}
        for d, kind in o["deps"].items():
            p = ops[d]
            if kind == "wait" and p["tok"] is None and (p["q"] not in top or pos[d] > pos[top[p["q"]]]): top[p["q"]] = d
        need.update(top.values())
        o["top"] = list(top.values())
        if o["grp"] is not None: lastg[o["grp"]] = o["id"]
    cnt = {}
    for o in order:
        if o["id"] in need:
            cnt[o["q"]] = cnt.get(o["q"], 0) + 1
            o["tok"] = (QSEM[o["q"]], cnt[o["q"]])
            o["inc"] = True
    known = {q: {} for q in qs}
    clock, sent, total = {}, 0, {}
    for o in order:
        q = o["q"]
        if q == "R":
            clock[o["id"]] = {o["tok"][0]: o["tok"][1]}
            total[o["tok"][0]] = o["tok"][1]
            continue
        kn = known[q]
        ds = o["top"] + [d for d, kind in o["deps"].items() if kind == "wait" and ops[d]["lat"] > 0]
        for d in sorted(ds, key=lambda d: -pos[d]):
            s, v = ops[d]["tok"]
            if kn.get(s, 0) < v:
                qs[q].wait_ge(T.sem[s], v)
                for s2, v2 in clock[d].items(): kn[s2] = max(kn.get(s2, 0), v2)
        if q == "P":
            for k, (out, l, r, start, stop) in enumerate(o["mm"]):
                if o["shared"]: stop = lastg[o["grp"]] == o["id"] and k == len(o["mm"]) - 1
                ins = g.tensor.matmul(out, l, r, start, stop)
        else:
            ins = o["fn"](g)
        ck = dict(kn)
        if o.get("inc"):
            ins.then_inc(T.sem[o["tok"][0]], 1)
        if isinstance(o["tok"], tuple):
            ck[o["tok"][0]] = o["tok"][1]
            total[o["tok"][0]] = o["tok"][1]
        clock[o["id"]] = ck
        sent += o.get("sent", 0)
    total["sent"] = sent
    for s, v in total.items():
        g.wait_ge(T.sem[s], v)


ORDER = []


def rank_program(g, core, T, topo):
    rank = T.rank_of(core)
    if rank is None:
        return
    ops = build(T, topo, core, rank)
    link(ops)
    if not ORDER:
        ORDER.extend(schedule(ops, [build(T, topo, core, rank, c) for c in COSTS])[0])
    emit(g, T, ops, [ops[i] for i in ORDER])
